import numpy as np
import ml_dtypes


def mxq(x, axis, fmt="e4m3"):
    dtype, down = {"e4m3": (ml_dtypes.float8_e4m3fn, 7), "e5m2": (ml_dtypes.float8_e5m2, 14)}[fmt]
    v = np.moveaxis(np.asarray(x, np.float32).astype(ml_dtypes.bfloat16).astype(np.float64), axis, -1)
    blocks = v.reshape(v.shape[:-1] + (-1, 32))
    amax = np.abs(blocks).max(-1, keepdims=True)
    byte = np.maximum(np.where(amax > 0, np.frexp(amax)[1] - 1 + 127, 0) - down, 1)
    scale = np.exp2(byte - 127.0)
    codes = (blocks / scale).astype(np.float32).astype(dtype).astype(np.float64)
    return np.moveaxis((codes * scale).reshape(v.shape), -1, axis)


WIDE = False


def mx_kscale(k):
    if not WIDE:
        return np.ones(k)
    levels = np.array([10, -10, 5, -5, 0])
    if k % 512:
        return np.exp2(np.random.permutation(np.resize(levels, k // 32))).repeat(32)
    a = np.empty((k // 512, 16))
    for p in range(k // 512):
        a[p, :8] = np.random.permutation(np.resize(levels, 8))
        for g in range(8):
            far = levels[np.abs(levels - a[p, g]) >= 10]
            a[p, g + 8] = far[np.random.randint(len(far))]
    return np.exp2(a.ravel()).repeat(32)


def f64(x):
    return np.asarray(x).astype(np.float64)


def striped(idx):
    return np.tile(idx.reshape(-1, 16).T, (8, 1)).astype(np.uint16)


def unstriped(offs):
    return offs[:16].T.reshape(-1).astype(np.int64)


def striped8(idx):
    return np.concatenate([x.reshape(-1, 16).T for x in idx]).astype(np.uint16)


def runs(offs, k):
    lists = np.stack([offs[16 * r : 16 * r + 16].T.reshape(-1) for r in range(8)]).astype(np.int64)
    return lists[np.arange(k) % 512 // 64]


def pack_weight(w):
    k, n = w.shape
    w = f64(np.asarray(w, np.float32).astype(ml_dtypes.bfloat16)).reshape(k // 32, 32, n)
    amax = np.abs(w).max(1)
    byte = np.clip(np.where(amax > 0, np.frexp(amax)[1] - 1 + 127 - 7, 1), 1, 254)
    scaled = (w * np.exp2(127.0 - byte)[:, None, :]).reshape(k, n).astype(np.float32)
    words = np.ascontiguousarray(scaled.reshape(k // 512, 128, 4, n).transpose(0, 1, 3, 2)).astype(ml_dtypes.float8_e4m3fn).view(np.uint8)
    return words, np.ascontiguousarray(byte.astype(np.uint8).reshape(k // 512, 16, n))


def unpack_weight(words, scales):
    g, p, n, _ = words.shape
    vals = np.ascontiguousarray(words).view(ml_dtypes.float8_e4m3fn).astype(np.float64) * np.repeat(np.exp2(scales.astype(np.float64) - 127.0), 8, axis=1)[..., None]
    return vals.transpose(0, 1, 3, 2).reshape(g * 512, n)


E2M1 = np.array([0.0, 0.5, 1.0, 1.5, 2.0, 3.0, 4.0, 6.0, -0.0, -0.5, -1.0, -1.5, -2.0, -3.0, -4.0, -6.0])


def pack_fp4(w):
    k, n = w.shape
    w = f64(np.asarray(w, np.float32).astype(ml_dtypes.bfloat16)).reshape(k // 32, 32, n)
    amax = np.abs(w).max(1)
    mant, ex = np.frexp(amax / 6.0)
    byte = np.clip(np.where(amax > 0, np.where(mant > 0.5, ex, ex - 1) + 127, 1), 1, 254)
    scaled = (w * np.exp2(127.0 - byte)[:, None, :]).reshape(k, n).astype(np.float32)
    c = np.ascontiguousarray(scaled.reshape(k // 512, 128, 4, n).transpose(0, 1, 3, 2)).astype(ml_dtypes.float4_e2m1fn).view(np.uint8) & 0xF
    words = (c[..., 0::2] | (c[..., 1::2] << 4)).reshape(k // 512, 128, 2 * n)
    return np.ascontiguousarray(words), np.ascontiguousarray(byte.astype(np.uint8).reshape(k // 512, 16, n))


def unpack_fp4(words, scales):
    g, _, n = scales.shape
    words = np.ascontiguousarray(words).reshape(g, 128, n, 2)
    nib = np.empty((g, 128, n, 4), np.uint8)
    nib[..., 0::2] = words & 0xF
    nib[..., 1::2] = words >> 4
    vals = E2M1[nib] * np.repeat(np.exp2(scales.astype(np.float64) - 127.0), 8, axis=1)[..., None]
    return vals.transpose(0, 1, 3, 2).reshape(g * 512, n)


def planes(y):
    n, m = y.shape
    v = y.astype(np.float32).astype(ml_dtypes.bfloat16).astype(np.float64).reshape(n // 32, 32, m)
    top = np.abs(v).max(1)
    byte = np.clip(np.where(top > 0, np.frexp(top)[1] - 1 + 127 - 7, 1), 1, 254)
    codes = (v * np.exp2(127.0 - byte)[:, None, :]).reshape(n, m).astype(np.float32).astype(ml_dtypes.float8_e4m3fn).view(np.uint8)
    words = codes.reshape(n // 512, 128, 4, m).transpose(0, 1, 3, 2)
    return np.ascontiguousarray(words), np.ascontiguousarray(byte.astype(np.uint8).reshape(n // 512, 16, m))


K, T, S, N, H = 512, 2048, 512, 512, 512


def setup_inputs():
    n = np.random.standard_normal
    s = mx_kscale(K)[:, None]
    u = mx_kscale(H)
    packed_xT = pack_weight(n((K, T)) * s)
    packed_w1 = pack_fp4(n((K, H)) / np.sqrt(K) / s)
    packed_w2 = pack_fp4(n((H, H)) / np.sqrt(H) / u[:, None])
    packed_w3 = pack_fp4(n((H, N)) / np.sqrt(H) / u[:, None])
    return {
        "x_words": packed_xT[0],
        "x_scales": packed_xT[1],
        "w1_words": packed_w1[0],
        "w1_scales": packed_w1[1],
        "gn": (np.random.uniform(0.5, 1.5, (H, 1)) * u[:, None]).astype(np.float32),
        "w2_words": packed_w2[0],
        "w2_scales": packed_w2[1],
        "res": n((N, S)).astype(np.float32),
        "w3_words": packed_w3[0],
        "w3_scales": packed_w3[1],
        "offs": striped(np.random.permutation(T)[:S]),
        "n1": striped8(np.stack([np.random.permutation(S) for _ in range(8)])),
        "n2": striped8(np.stack([np.random.permutation(S) for _ in range(8)])),
        "mv": striped8(np.stack([np.random.permutation(S) for _ in range(8)])),
    }


def reference(x_words, x_scales, w1_words, w1_scales, gn, w2_words, w2_scales, res, w3_words, w3_scales, offs, n1, n2, mv):
    xq = unpack_weight(x_words, x_scales)[:, unstriped(offs)]
    y = unpack_fp4(w1_words, w1_scales).T @ xq
    a = y - (y[np.arange(H)[:, None], runs(n1, H)])
    b = y - (y[np.arange(H)[:, None], runs(n2, H)])
    z = f64(gn) * (np.log(np.exp(a) + np.exp(-1.0 * a)) - (np.log(np.exp(b) + np.exp(-1.0 * b))))
    h = np.tanh(unpack_fp4(w2_words, w2_scales).T @ mxq(z, 0, "e4m3"))
    z2 = f64(gn) * (h[np.arange(H)[:, None], runs(mv, H)])
    out_0 = f64(res) + (unpack_fp4(w3_words, w3_scales).T @ mxq(z2, 0, "e4m3"))
    return (out_0,) + planes(out_0)

@@ -1,0 +1,231 @@
+from contextlib import ExitStack
+
+import concourse.mybir as mybir
+
+F32 = mybir.dt.float32
+BF16 = mybir.dt.bfloat16
+I32 = mybir.dt.int32
+U32 = mybir.dt.uint32
+U16 = mybir.dt.uint16
+U8 = mybir.dt.uint8
+FP8X4 = mybir.dt.float8_e4m3fn_x4
+FP4X4 = mybir.dt.float4_e2m1fn_x4
+ACT = mybir.ActivationFunctionType
+ALU = mybir.AluOpType
+
+P = 128
+PACK = 4
+T = 2048
+S = 512
+HALF = 256
+BLK = 128
+PIECES = ((0, 256), (256, 128), (384, 128))
+FLOPS = 3 * 2 * 512 * 512 * 512
+
+
+def tile_picked_logcosh2_none_po_kernel(
+    tc, x_words, x_scales, w1_words, w1_scales, gn, w2_words, w2_scales, res, w3_words, w3_scales,
+    offs, n1, n2, mv, out_0, out_1, out_2,
+):
+    nc = tc.nc
+    with ExitStack() as ctx:
+        sb = ctx.enter_context(tc.tile_pool(name="sb", bufs=1))
+        ps = ctx.enter_context(tc.psum_pool(name="ps", bufs=1))
+
+        def sbt(name, shape, dtype):
+            return sb.tile(shape, dtype, name=name, align_bytes=64)
+
+        def bank(i, name):
+            return ps.tile([P, 512], F32, name=name, tag="bank%d" % i)
+
+        def load_list(name, src):
+            tile = sb.tile([P, S // 16], U16, name=name)
+            nc.sync.dma_start(tile[:], src)
+            return tile
+
+        def load_scale_rows(queue, tile, src, quadrants):
+            for q in quadrants:
+                queue.dma_start(tile[32 * q : 32 * q + 4, :].bitcast(I32), src[0, 4 * q : 4 * q + 4, :].bitcast(I32))
+
+        def zeroed(name, width, engine):
+            tile = sbt(name, [P, width], U8)
+            engine.memset(tile[:].bitcast(I32), 0)
+            return tile
+
+        def deal_words(name, raw_words):
+            words = sbt(name, [P, PACK * P * 2], U8)
+            nc.vector.tensor_copy(
+                out=words[:].rearrange("p (t c i b) -> p c t i b", t=PACK, i=8, b=2),
+                in_=raw_words[:].rearrange("p (c i t b) -> p c t i b", t=PACK, i=8, b=2),
+            )
+            return words
+
+        def deal_scales(name, raw_scales, n):
+            scales = sbt(name, [P, n * S], U8)
+            nc.vector.tensor_copy(
+                out=scales[:].rearrange("p (w t m) -> p w t m", w=n, t=PACK),
+                in_=raw_scales.rearrange("p (w m t) -> p w t m", w=n, t=PACK),
+            )
+            return scales
+
+        def load_words(name, src, tag=""):
+            tile = sb.tile([P, 1024], U8, name=name, tag=tag, align_bytes=64)
+            nc.sync.dma_start(tile[:].bitcast(I32), src[0].bitcast(I32))
+            return tile
+
+        def product(out, w, t, codes, scales):
+            nc.tensor.matmul_mx(
+                out=out,
+                lhsT=w[0][:, 2 * P * t : 2 * P * (t + 1)].bitcast(FP4X4),
+                lhsT_scale=w[1][:, P * t : P * (t + 1)],
+                rhs=codes.bitcast(FP8X4),
+                rhs_scale=scales,
+                start=True,
+                stop=True,
+            )
+
+        def cols(lst, start, n):
+            return lst[:, start // 16 : (start + n) // 16]
+
+        w1s_raw = zeroed("w1s_raw", S, nc.vector)[:]
+        xs_all = zeroed("xs_all", T, nc.vector)
+        ws_raw = zeroed("ws_raw", 2 * S, nc.vector)
+        w2s_raw, w3s_raw = (ws_raw[:, i * S : (i + 1) * S] for i in range(2))
+        offs_t = load_list("offs_t", offs)
+        w1w_raw = load_words("w1w_raw", w1_words)
+        load_scale_rows(nc.sync, w1s_raw, w1_scales, [0])
+        xw_all = sbt("xw_all", [P, T], I32)
+        nc.sync.dma_start(xw_all[:], x_words[0].rearrange("p c r -> p (c r)").bitcast(I32))
+        load_scale_rows(nc.sync, xs_all[:], x_scales, range(4))
+        load_scale_rows(nc.sync, w1s_raw, w1_scales, [1, 2, 3])
+        n1_t = load_list("n1_t", n1)
+        n2_t = load_list("n2_t", n2)
+        w2w_raw = load_words("w2w_raw", w2_words)
+        load_scale_rows(nc.sync, w2s_raw, w2_scales, range(4))
+        load_scale_rows(nc.sync, w3s_raw, w3_scales, range(4))
+        gain = sbt("gain", [P, PACK], F32)
+        nc.sync.dma_start(gain[:], gn.rearrange("(p t) o -> p (t o)", t=PACK))
+        mv_t = load_list("mv_t", mv)
+        res_t = sbt("res_t", [P, PACK, S], F32)
+        nc.sync.dma_start(res_t[:], res.rearrange("(p t) s -> p t s", t=PACK))
+
+        y_two = [sbt("y_two%d" % t, [P, 2 * S], F32) for t in range(PACK + 1)]
+        nc.vector.memset(y_two[0][:, S:], 0.0)
+        w1 = (deal_words("w1w", w1w_raw), deal_scales("w1s", w1s_raw, 1))
+        xs = sbt("xs", [P, S], U8)
+        nc.vector.tensor_copy(out=xs[:], in_=xs_all[:].indirect(offs_t[:]))
+        xw = sbt("xw", [P, S], U32)
+        y_ps = {}
+        for h in range(2):
+            tok = slice(h * HALF, (h + 1) * HALF)
+            nc.vector.tensor_copy(out=xw[:, tok], in_=xw_all[:].bitcast(U32).indirect(cols(offs_t, h * HALF, HALF)))
+            for t in range(PACK):
+                y_ps[h, t] = bank(4 * h + t, "y_ps%d_%d" % (h, t))
+                product(y_ps[h, t][:, :HALF], w1, t, xw[:, tok], xs[:, tok])
+
+        ab = sbt("ab", [P, PACK, 2, S], F32)
+        mag = sbt("mag", [P, PACK, 2, S], F32)
+        th = sbt("th", [P, PACK, 2, S], F32)
+        for t in range(PACK):
+            for h in range(2):
+                tok = slice(h * HALF, (h + 1) * HALF)
+                nc.scalar.copy(out=y_two[t][:, tok], in_=y_ps[h, t][:, :HALF])
+            if t < 2:
+                nc.vector.tensor_copy(out=y_two[t + 1][:, S:], in_=y_two[t][:, :S])
+            else:
+                nc.sync.dma_start(y_two[t + 1][:, S:], y_two[t][:, :S])
+        for t in range(PACK):
+            for j, lst in enumerate((n1_t, n2_t)):
+                nc.vector.tensor_tensor(
+                    out=ab[:, t, j, :], in0=y_two[t][:].indirect(lst[:]), in1=y_two[t + 1][:, S:], op=ALU.subtract
+                )
+                nc.scalar.activation(out=mag[:, t, j, :], in_=ab[:, t, j, :], func=ACT.Abs)
+                nc.scalar.activation(out=th[:, t, j, :], in_=mag[:, t, j, :], func=ACT.Tanh)
+        w2w = deal_words("w2w", w2w_raw)
+        w23s = deal_scales("w23s", ws_raw[:], 2)
+        w2 = (w2w, w23s[:, :S])
+        gain_rows = sbt("gain_rows", [P, PACK, HALF], F32)
+        nc.vector.tensor_copy(out=gain_rows[:], in_=gain[:].unsqueeze(2).broadcast_to([P, PACK, HALF]))
+
+        part = []
+        for h in range(2):
+            tok = slice(h * HALF, (h + 1) * HALF)
+            diff = sbt("diff%d" % h, [P, PACK, HALF], F32)
+            nc.vector.tensor_tensor(out=diff[:], in0=mag[:, :, 0, tok], in1=mag[:, :, 1, tok], op=ALU.subtract)
+            log_a = sb.tile([P, PACK, HALF], F32, name="log_a%d" % h, tag="log_a%d" % h, align_bytes=64)
+            nc.scalar.activation(out=log_a[:], in_=th[:, :, 0, tok], func=ACT.Ln, bias=1.0)
+            part.append((diff, log_a))
+        log_b = []
+        for k, (lo, n) in enumerate(PIECES):
+            lg = sbt("log_b%d" % k, [P, PACK, n], F32)
+            nc.scalar.activation(out=lg[:], in_=th[:, :, 1, lo : lo + n], func=ACT.Ln, bias=1.0)
+            log_b.append(lg)
+        less_a = sbt("less_a", [P, PACK, S], F32)
+        for h in range(2):
+            nc.vector.tensor_tensor(
+                out=less_a[:, :, h * HALF : (h + 1) * HALF], in0=part[h][0][:], in1=part[h][1][:], op=ALU.subtract
+            )
+        w3w_raw = load_words("w3w_raw", w3_words, tag="log_a1")
+
+        def woven(ap):
+            return ap.rearrange("p (c i t) -> p c t i", i=4, t=PACK)
+
+        def planes(ap):
+            return ap.rearrange("p t (c i) -> p c t i", i=4)
+
+        def banks_for(first, n, name):
+            per = 512 // n
+            tiles = [bank(first + i, "%s_%d" % (name, i)) for i in range(PACK // per)]
+            return tiles, [tiles[t // per][:, (t % per) * n : (t % per + 1) * n] for t in range(PACK)]
+
+        h_win = [sbt("h_win%d" % t, [P, S], F32) for t in range(PACK)]
+        for k, (lo, n) in enumerate(PIECES):
+            tok = slice(lo, lo + n)
+            u = sbt("u%d" % k, [P, PACK, n], F32)
+            nc.vector.tensor_tensor(out=u[:], in0=less_a[:, :, tok], in1=log_b[k][:], op=ALU.add)
+            z = sbt("z%d" % k, [P, n * PACK], BF16)
+            gain_b = gain[:].unsqueeze(1).unsqueeze(3).broadcast_to([P, n // 4, PACK, 4])
+            nc.vector.tensor_tensor(out=woven(z[:]), in0=planes(u[:]), in1=gain_b, op=ALU.mult)
+            zc = sbt("zc%d" % k, [P, n], U32)
+            zs = sbt("zs%d" % k, [P, n], U8)
+            nc.vector.quantize_mx(out=zc[:].bitcast(FP8X4), scales=zs[:], in_=z[:])
+            tiles, outs = banks_for(lo // BLK, n, "h_ps%d" % k)
+            for t in range(PACK):
+                product(outs[t], w2, t, zc[:], zs[:])
+            for t in range(PACK):
+                nc.scalar.activation(out=h_win[t][:, tok], in_=outs[t], func=ACT.Tanh)
+
+        w3 = (deal_words("w3w", w3w_raw), w23s[:, S:])
+        out_rows = out_0.rearrange("(p t) s -> p t s", t=PACK)
+        out_words = out_1[0].rearrange("p c r -> p (c r)").bitcast(I32)
+        oc = sbt("oc", [P, S], I32)
+        osc = sbt("osc", [P, S], U8)
+        for k, (lo, n) in enumerate(PIECES):
+            tok = slice(lo, lo + n)
+            g = sbt("g%d" % k, [P, PACK, n], F32)
+            for t in range(PACK):
+                nc.vector.tensor_tensor(
+                    out=g[:, t, :], in0=h_win[t][:].indirect(cols(mv_t, lo, n)), in1=gain_rows[:, t, :n], op=ALU.mult
+                )
+            z2 = sbt("z2_%d" % k, [P, n * PACK], BF16)
+            nc.scalar.copy(out=woven(z2[:]), in_=planes(g[:]))
+            z2c = sbt("z2c%d" % k, [P, n], U32)
+            z2s = sbt("z2s%d" % k, [P, n], U8)
+            nc.vector.quantize_mx(out=z2c[:].bitcast(FP8X4), scales=z2s[:], in_=z2[:])
+            tiles, outs = banks_for(4 + lo // BLK, n, "o_ps%d" % k)
+            for t in range(PACK):
+                product(outs[t], w3, t, z2c[:], z2s[:])
+            o = sbt("o%d" % k, [P, PACK, n], F32)
+            per = 512 // n
+            for i, tile in enumerate(tiles):
+                rows = slice(i * per, (i + 1) * per)
+                nc.vector.tensor_tensor(
+                    out=o[:, rows, :], in0=tile[:].rearrange("p (t s) -> p t s", t=per), in1=res_t[:, rows, tok], op=ALU.add
+                )
+            nc.sync.dma_start(out_rows[:, :, tok], o[:])
+            ob = sbt("ob%d" % k, [P, n * PACK], BF16)
+            nc.scalar.copy(out=woven(ob[:]), in_=planes(o[:]))
+            nc.vector.quantize_mx(out=oc[:, tok].bitcast(FP8X4), scales=osc[:, tok], in_=ob[:])
+            nc.sync.dma_start(out_words[:, tok], oc[:, tok])
+        for q in range(4):
+            (nc.sync if q % 2 else nc.scalar).dma_start(out_2[0, 4 * q : 4 * q + 4, :].bitcast(I32), osc[32 * q : 32 * q + 4, :].bitcast(I32))

@@ -1,6 +1,7 @@
 from contextlib import ExitStack
 
 import concourse.mybir as mybir
+from concourse.masks import make_identity
 
 F32 = mybir.dt.float32
 BF16 = mybir.dt.bfloat16
@@ -19,6 +20,7 @@ T = 2048
 S = 512
 HALF = 256
 BLK = 128
+LOG_ORDER = ((0, 0), (0, 1), (1, 0), (0, 2), (1, 1), (0, 3), (1, 2), (1, 3))
 PIECES = ((0, 256), (256, 128), (384, 128))
 FLOPS = 3 * 2 * 512 * 512 * 512
 
@@ -32,8 +34,8 @@ def tile_picked_logcosh2_none_po_kernel(
         sb = ctx.enter_context(tc.tile_pool(name="sb", bufs=1))
         ps = ctx.enter_context(tc.psum_pool(name="ps", bufs=1))
 
-        def sbt(name, shape, dtype):
-            return sb.tile(shape, dtype, name=name, align_bytes=64)
+        def sbt(name, shape, dtype, tag=""):
+            return sb.tile(shape, dtype, name=name, tag=tag, align_bytes=64)
 
         def bank(i, name):
             return ps.tile([P, 512], F32, name=name, tag="bank%d" % i)
@@ -47,22 +49,22 @@ def tile_picked_logcosh2_none_po_kernel(
             for q in quadrants:
                 queue.dma_start(tile[32 * q : 32 * q + 4, :].bitcast(I32), src[0, 4 * q : 4 * q + 4, :].bitcast(I32))
 
-        def zeroed(name, width, engine):
-            tile = sbt(name, [P, width], U8)
+        def zeroed(name, width, engine, tag=""):
+            tile = sbt(name, [P, width], U8, tag)
             engine.memset(tile[:].bitcast(I32), 0)
             return tile
 
-        def deal_words(name, raw_words):
-            words = sbt(name, [P, PACK * P * 2], U8)
+        def deal_words(name, raw_words, tag=""):
+            words = sbt(name, [P, PACK * P * 2], U8, tag)
             nc.vector.tensor_copy(
                 out=words[:].rearrange("p (t c i b) -> p c t i b", t=PACK, i=8, b=2),
                 in_=raw_words[:].rearrange("p (c i t b) -> p c t i b", t=PACK, i=8, b=2),
             )
             return words
 
-        def deal_scales(name, raw_scales, n):
-            scales = sbt(name, [P, n * S], U8)
-            nc.vector.tensor_copy(
+        def deal_scales(name, raw_scales, n, engine, tag=""):
+            scales = sbt(name, [P, n * S], U8, tag)
+            engine.tensor_copy(
                 out=scales[:].rearrange("p (w t m) -> p w t m", w=n, t=PACK),
                 in_=raw_scales.rearrange("p (w m t) -> p w t m", w=n, t=PACK),
             )
@@ -87,85 +89,121 @@ def tile_picked_logcosh2_none_po_kernel(
         def cols(lst, start, n):
             return lst[:, start // 16 : (start + n) // 16]
 
-        w1s_raw = zeroed("w1s_raw", S, nc.vector)[:]
-        xs_all = zeroed("xs_all", T, nc.vector)
+        xs_all = sbt("xs_all", [P, T], U8)
+        nc.vector.memset(xs_all[:, : 3 * T // 4].bitcast(I32), 0)
+        nc.gpsimd.memset(xs_all[:, 3 * T // 4 :].bitcast(I32), 0)
+        w1s_raw = zeroed("w1s_raw", S, nc.gpsimd, "w1s_raw")[:]
         ws_raw = zeroed("ws_raw", 2 * S, nc.vector)
         w2s_raw, w3s_raw = (ws_raw[:, i * S : (i + 1) * S] for i in range(2))
         offs_t = load_list("offs_t", offs)
-        w1w_raw = load_words("w1w_raw", w1_words)
-        load_scale_rows(nc.sync, w1s_raw, w1_scales, [0])
-        xw_all = sbt("xw_all", [P, T], I32)
-        nc.sync.dma_start(xw_all[:], x_words[0].rearrange("p c r -> p (c r)").bitcast(I32))
+        w1w_raw = load_words("w1w_raw", w1_words, "w_raw")
         load_scale_rows(nc.sync, xs_all[:], x_scales, range(4))
-        load_scale_rows(nc.sync, w1s_raw, w1_scales, [1, 2, 3])
+        xw_all = sbt("xw_all", [P, T], I32, "big")
+        nc.sync.dma_start(xw_all[:], x_words[0].rearrange("p c r -> p (c r)").bitcast(I32))
+        load_scale_rows(nc.sync, w1s_raw, w1_scales, range(4))
         n1_t = load_list("n1_t", n1)
         n2_t = load_list("n2_t", n2)
-        w2w_raw = load_words("w2w_raw", w2_words)
-        load_scale_rows(nc.sync, w2s_raw, w2_scales, range(4))
-        load_scale_rows(nc.sync, w3s_raw, w3_scales, range(4))
-        gain = sbt("gain", [P, PACK], F32)
-        nc.sync.dma_start(gain[:], gn.rearrange("(p t) o -> p (t o)", t=PACK))
-        mv_t = load_list("mv_t", mv)
-        res_t = sbt("res_t", [P, PACK, S], F32)
-        nc.sync.dma_start(res_t[:], res.rearrange("(p t) s -> p t s", t=PACK))
+        ident = sbt("ident", [P, P], F32)
+        make_identity(nc, ident[:])
 
-        y_two = [sbt("y_two%d" % t, [P, 2 * S], F32) for t in range(PACK + 1)]
+        y_two = [sbt("y_two%d" % t, [P, 2 * S], F32, "y_two%d" % t) for t in range(PACK + 1)]
         nc.vector.memset(y_two[0][:, S:], 0.0)
-        w1 = (deal_words("w1w", w1w_raw), deal_scales("w1s", w1s_raw, 1))
+        w1 = (deal_words("w1w", w1w_raw), deal_scales("w1s", w1s_raw, 1, nc.gpsimd))
         xs = sbt("xs", [P, S], U8)
-        nc.vector.tensor_copy(out=xs[:], in_=xs_all[:].indirect(offs_t[:]))
         xw = sbt("xw", [P, S], U32)
         y_ps = {}
         for h in range(2):
             tok = slice(h * HALF, (h + 1) * HALF)
+            nc.vector.tensor_copy(out=xs[:, tok], in_=xs_all[:].indirect(cols(offs_t, h * HALF, HALF)))
             nc.vector.tensor_copy(out=xw[:, tok], in_=xw_all[:].bitcast(U32).indirect(cols(offs_t, h * HALF, HALF)))
             for t in range(PACK):
                 y_ps[h, t] = bank(4 * h + t, "y_ps%d_%d" % (h, t))
                 product(y_ps[h, t][:, :HALF], w1, t, xw[:, tok], xs[:, tok])
 
-        ab = sbt("ab", [P, PACK, 2, S], F32)
+        w2w_raw = load_words("w2w_raw", w2_words, "w_raw")
+        gain = sbt("gain", [P, PACK], F32, "w1s_raw")
+        nc.sync.dma_start(gain[:], gn.rearrange("(p t) o -> p (t o)", t=PACK))
+        load_scale_rows(nc.sync, w2s_raw, w2_scales, range(4))
+        load_scale_rows(nc.sync, w3s_raw, w3_scales, range(4))
+        mv_t = load_list("mv_t", mv)
+
+        ab = sbt("ab", [P, PACK, 2, S], F32, "ab")
         mag = sbt("mag", [P, PACK, 2, S], F32)
+        neg_b = sbt("neg_b", [P, PACK, S], F32)
         th = sbt("th", [P, PACK, 2, S], F32)
         for t in range(PACK):
-            for h in range(2):
-                tok = slice(h * HALF, (h + 1) * HALF)
-                nc.scalar.copy(out=y_two[t][:, tok], in_=y_ps[h, t][:, :HALF])
-            if t < 2:
-                nc.vector.tensor_copy(out=y_two[t + 1][:, S:], in_=y_two[t][:, :S])
+            nc.scalar.copy(out=y_two[t][:, :HALF], in_=y_ps[0, t][:, :HALF])
+            if t == 0:
+                nc.scalar.copy(out=y_two[1][:, S : S + HALF], in_=y_ps[0, 0][:, :HALF])
+        for t in range(PACK):
+            nc.scalar.copy(out=y_two[t][:, HALF:S], in_=y_ps[1, t][:, :HALF])
+            if t == 0:
+                nc.vector.tensor_copy(out=y_two[1][:, S + HALF :], in_=y_two[0][:, HALF:S])
             else:
                 nc.sync.dma_start(y_two[t + 1][:, S:], y_two[t][:, :S])
+        res_t = sbt("res_t", [P, PACK, S], F32, "big")
+        nc.sync.dma_start(res_t[:], res.rearrange("(p t) s -> p t s", t=PACK))
         for t in range(PACK):
             for j, lst in enumerate((n1_t, n2_t)):
-                nc.vector.tensor_tensor(
-                    out=ab[:, t, j, :], in0=y_two[t][:].indirect(lst[:]), in1=y_two[t + 1][:, S:], op=ALU.subtract
+                n = HALF if (t, j) == (PACK - 1, 1) else S
+                for lo in range(0, S, n):
+                    nc.vector.tensor_tensor(
+                        out=ab[:, t, j, lo : lo + n],
+                        in0=y_two[t][:].indirect(cols(lst, lo, n)),
+                        in1=y_two[t + 1][:, S + lo : S + lo + n],
+                        op=ALU.subtract,
+                    )
+            if t == 0:
+                nc.scalar.activation(out=mag[:, t, 0, :], in_=ab[:, t, 0, :], func=ACT.Abs)
+                nc.vector.scalar_tensor_tensor(
+                    out=mag[:, t, 1, :], in0=ab[:, t, 1, :], scalar=-1.0, in1=ab[:, t, 1, :], op0=ALU.mult, op1=ALU.max
                 )
-                nc.scalar.activation(out=mag[:, t, j, :], in_=ab[:, t, j, :], func=ACT.Abs)
-                nc.scalar.activation(out=th[:, t, j, :], in_=mag[:, t, j, :], func=ACT.Tanh)
-        w2w = deal_words("w2w", w2w_raw)
-        w23s = deal_scales("w23s", ws_raw[:], 2)
-        w2 = (w2w, w23s[:, :S])
-        gain_rows = sbt("gain_rows", [P, PACK, HALF], F32)
-        nc.vector.tensor_copy(out=gain_rows[:], in_=gain[:].unsqueeze(2).broadcast_to([P, PACK, HALF]))
+                nc.scalar.activation(out=th[:, t, 0, :], in_=mag[:, t, 0, :], func=ACT.Tanh)
+                nc.scalar.activation(out=th[:, t, 1, :], in_=mag[:, t, 1, :], func=ACT.Tanh)
+            elif t < PACK - 1:
+                nc.scalar.activation(out=mag[:, t, :, :], in_=ab[:, t, :, :], func=ACT.Abs)
+                nc.scalar.activation(out=th[:, t, :, :], in_=mag[:, t, :, :], func=ACT.Tanh)
+            else:
+                parts = ((0, 0, S), (1, 0, HALF), (1, HALF, S))
+                for j, lo, hi in parts:
+                    nc.scalar.activation(out=mag[:, t, j, lo:hi], in_=ab[:, t, j, lo:hi], func=ACT.Abs)
+                for j, lo, hi in parts:
+                    nc.scalar.activation(out=th[:, t, j, lo:hi], in_=mag[:, t, j, lo:hi], func=ACT.Tanh)
+        turned = (S // BLK - 1) * BLK
+        nc.vector.tensor_scalar(
+            out=neg_b[:, :, :turned], in0=mag[:, :, 1, :turned], scalar1=-1.0, scalar2=None, op0=ALU.mult
+        )
+        last_diff = sbt("last_diff", [P, PACK, BLK], F32)
+        nc.vector.tensor_tensor(out=last_diff[:], in0=mag[:, :, 0, turned:], in1=mag[:, :, 1, turned:], op=ALU.subtract)
 
-        part = []
-        for h in range(2):
-            tok = slice(h * HALF, (h + 1) * HALF)
-            diff = sbt("diff%d" % h, [P, PACK, HALF], F32)
-            nc.vector.tensor_tensor(out=diff[:], in0=mag[:, :, 0, tok], in1=mag[:, :, 1, tok], op=ALU.subtract)
-            log_a = sb.tile([P, PACK, HALF], F32, name="log_a%d" % h, tag="log_a%d" % h, align_bytes=64)
-            nc.scalar.activation(out=log_a[:], in_=th[:, :, 0, tok], func=ACT.Ln, bias=1.0)
-            part.append((diff, log_a))
-        log_b = []
-        for k, (lo, n) in enumerate(PIECES):
-            lg = sbt("log_b%d" % k, [P, PACK, n], F32)
-            nc.scalar.activation(out=lg[:], in_=th[:, :, 1, lo : lo + n], func=ACT.Ln, bias=1.0)
-            log_b.append(lg)
-        less_a = sbt("less_a", [P, PACK, S], F32)
-        for h in range(2):
-            nc.vector.tensor_tensor(
-                out=less_a[:, :, h * HALF : (h + 1) * HALF], in0=part[h][0][:], in1=part[h][1][:], op=ALU.subtract
-            )
-        w3w_raw = load_words("w3w_raw", w3_words, tag="log_a1")
+        g_ps = bank(0, "g_ps")
+        for t in range(PACK):
+            nc.tensor.transpose(g_ps[:, t * P : (t + 1) * P], gain[:, t : t + 1].to_broadcast([P, P]), ident[:])
+        gains = sbt("gains", [P, S + PACK * HALF], F32, "ab")
+        gain_free = gains[:, :S].rearrange("s (u p e) -> s u p e", u=2, e=2)
+        nc.vector.tensor_copy(out=gain_free, in_=g_ps[:].rearrange("s (u e p) -> s u p e", u=2, e=2))
+        w2w = deal_words("w2w", w2w_raw, "y_two4")
+        w23s = deal_scales("w23s", ws_raw[:], 2, nc.vector, "y_two3")
+        w2 = (w2w, w23s[:, :S])
+
+        blocks = S // BLK
+        logs = {}
+        for j, k in LOG_ORDER:
+            logs[j, k] = sbt("log%d_%d" % (j, k), [P, PACK, BLK], F32, "log%d_%d" % (j, k))
+            nc.scalar.activation(out=logs[j, k][:], in_=th[:, :, j, k * BLK : (k + 1) * BLK], func=ACT.Ln, bias=1.0)
+        w3w_raw = load_words("w3w_raw", w3_words, "w_raw")
+
+        sums = [bank(4 + k, "sums%d" % k) for k in range(blocks - 1)]
+
+        def add_turned(k, t, src, start=False, stop=False):
+            nc.tensor.matmul(sums[k][:, t * P : (t + 1) * P], src, ident[:], start=start, stop=stop, is_transpose=True)
+
+        for t in range(PACK):
+            for k in range(blocks - 1):
+                add_turned(k, t, mag[:, t, 0, k * BLK : (k + 1) * BLK], start=(t == 0))
+        for k in range(blocks - 1):
+            for t in range(PACK):
+                add_turned(k, t, neg_b[:, t, k * BLK : (k + 1) * BLK])
 
         def woven(ap):
             return ap.rearrange("p (c i t) -> p c t i", i=4, t=PACK)
@@ -179,23 +217,69 @@ def tile_picked_logcosh2_none_po_kernel(
             return tiles, [tiles[t // per][:, (t % per) * n : (t % per + 1) * n] for t in range(PACK)]
 
         h_win = [sbt("h_win%d" % t, [P, S], F32) for t in range(PACK)]
-        for k, (lo, n) in enumerate(PIECES):
-            tok = slice(lo, lo + n)
-            u = sbt("u%d" % k, [P, PACK, n], F32)
-            nc.vector.tensor_tensor(out=u[:], in0=less_a[:, :, tok], in1=log_b[k][:], op=ALU.add)
-            z = sbt("z%d" % k, [P, n * PACK], BF16)
-            gain_b = gain[:].unsqueeze(1).unsqueeze(3).broadcast_to([P, n // 4, PACK, 4])
-            nc.vector.tensor_tensor(out=woven(z[:]), in0=planes(u[:]), in1=gain_b, op=ALU.mult)
-            zc = sbt("zc%d" % k, [P, n], U32)
-            zs = sbt("zs%d" % k, [P, n], U8)
-            nc.vector.quantize_mx(out=zc[:].bitcast(FP8X4), scales=zs[:], in_=z[:])
-            tiles, outs = banks_for(lo // BLK, n, "h_ps%d" % k)
+        z_turned, z_woven = {}, {}
+
+        def take_log_a(k):
+            neg = sbt("neg_log%d" % k, [P, PACK, BLK], F32)
+            nc.vector.tensor_scalar(out=neg[:], in0=logs[0, k][:], scalar1=-1.0, scalar2=None, op0=ALU.mult)
+            for t in range(PACK):
+                add_turned(k, t, neg[:, t, :])
+
+        def close_sum(k):
+            for t in range(PACK):
+                add_turned(k, t, logs[1, k][:, t, :], stop=(t == PACK - 1))
+            z_turned[k] = sbt("z_turned%d" % k, [P, 2, P, 2], BF16)
+            nc.vector.tensor_tensor(
+                out=z_turned[k][:], in0=sums[k][:].rearrange("s (u e p) -> s u p e", u=2, e=2), in1=gain_free, op=ALU.mult
+            )
+
+        def turn_back(k):
+            pairs = z_turned[k][:].rearrange("s u p e -> s (u p e)").bitcast(F32)
+            back = bank(k, "back%d" % k)
+            for u in range(2):
+                nc.tensor.transpose(back[:, u * P : (u + 1) * P], pairs[:, u * P : (u + 1) * P], ident[:])
+            z_woven[k] = sbt("z%d" % k, [P, BLK * PACK], BF16)
+            nc.vector.tensor_copy(
+                out=z_woven[k][:].bitcast(F32).rearrange("p (s u) -> p s u", u=2),
+                in_=back[:, : 2 * P].rearrange("p (u s) -> p s u", u=2),
+            )
+
+        def second_product(k):
+            zc = sbt("zc%d" % k, [P, BLK], U32)
+            zs = sbt("zs%d" % k, [P, BLK], U8)
+            nc.vector.quantize_mx(out=zc[:].bitcast(FP8X4), scales=zs[:], in_=z_woven[k][:])
+            tiles, outs = banks_for(4 + k, BLK, "h_ps%d" % k)
             for t in range(PACK):
                 product(outs[t], w2, t, zc[:], zs[:])
             for t in range(PACK):
-                nc.scalar.activation(out=h_win[t][:, tok], in_=outs[t], func=ACT.Tanh)
+                nc.scalar.activation(out=h_win[t][:, k * BLK : (k + 1) * BLK], in_=outs[t], func=ACT.Tanh)
 
-        w3 = (deal_words("w3w", w3w_raw), w23s[:, S:])
+        last = blocks - 1
+        last_part = sbt("last_part", [P, PACK, BLK], F32)
+        last_sum = sbt("last_sum", [P, PACK, BLK], F32)
+
+        def last_log_a(k):
+            nc.vector.tensor_tensor(out=last_part[:], in0=last_diff[:], in1=logs[0, k][:], op=ALU.subtract)
+
+        def last_close(k):
+            nc.vector.tensor_tensor(out=last_sum[:], in0=last_part[:], in1=logs[1, k][:], op=ALU.add)
+
+        def last_weave(k):
+            z_woven[k] = sbt("z%d" % k, [P, BLK * PACK], BF16)
+            gain_b = gain[:].unsqueeze(1).unsqueeze(3).broadcast_to([P, BLK // 4, PACK, 4])
+            nc.vector.tensor_tensor(out=woven(z_woven[k][:]), in0=planes(last_sum[:]), in1=gain_b, op=ALU.mult)
+
+        stages = (take_log_a, close_sum, turn_back, second_product)
+        last_stages = (last_log_a, last_close, last_weave, second_product)
+        for step in range(blocks + len(stages) - 1):
+            for i in range(len(stages)):
+                k = step - i
+                if 0 <= k < blocks:
+                    (last_stages if k == last else stages)[i](k)
+
+        gain_rows = gains[:, S:].rearrange("p (t s) -> p t s", t=PACK)
+        nc.vector.tensor_copy(out=gain_rows, in_=gain[:].unsqueeze(2).broadcast_to([P, PACK, HALF]))
+        w3 = (deal_words("w3w", w3w_raw, "log1_1"), w23s[:, S:])
         out_rows = out_0.rearrange("(p t) s -> p t s", t=PACK)
         out_words = out_1[0].rearrange("p c r -> p (c r)").bitcast(I32)
         oc = sbt("oc", [P, S], I32)
@@ -207,12 +291,12 @@ def tile_picked_logcosh2_none_po_kernel(
                 nc.vector.tensor_tensor(
                     out=g[:, t, :], in0=h_win[t][:].indirect(cols(mv_t, lo, n)), in1=gain_rows[:, t, :n], op=ALU.mult
                 )
-            z2 = sbt("z2_%d" % k, [P, n * PACK], BF16)
+            z2 = sbt("z2_%d" % k, [P, n * PACK], BF16, "z2_%d" % k)
             nc.scalar.copy(out=woven(z2[:]), in_=planes(g[:]))
             z2c = sbt("z2c%d" % k, [P, n], U32)
             z2s = sbt("z2s%d" % k, [P, n], U8)
             nc.vector.quantize_mx(out=z2c[:].bitcast(FP8X4), scales=z2s[:], in_=z2[:])
-            tiles, outs = banks_for(4 + lo // BLK, n, "o_ps%d" % k)
+            tiles, outs = banks_for(lo // BLK, n, "o_ps%d" % k)
             for t in range(PACK):
                 product(outs[t], w3, t, z2c[:], z2s[:])
             o = sbt("o%d" % k, [P, PACK, n], F32)
@@ -224,7 +308,10 @@ def tile_picked_logcosh2_none_po_kernel(
                 )
             nc.sync.dma_start(out_rows[:, :, tok], o[:])
             ob = sbt("ob%d" % k, [P, n * PACK], BF16)
-            nc.scalar.copy(out=woven(ob[:]), in_=planes(o[:]))
+            if k == 2:
+                nc.vector.tensor_copy(out=woven(ob[:]), in_=planes(o[:]))
+            else:
+                nc.scalar.copy(out=woven(ob[:]), in_=planes(o[:]))
             nc.vector.quantize_mx(out=oc[:, tok].bitcast(FP8X4), scales=osc[:, tok], in_=ob[:])
             nc.sync.dma_start(out_words[:, tok], oc[:, tok])
         for q in range(4):

@@ -1,7 +1,6 @@
 from contextlib import ExitStack
 
 import concourse.mybir as mybir
-from concourse.masks import make_identity
 
 F32 = mybir.dt.float32
 BF16 = mybir.dt.bfloat16
@@ -20,7 +19,7 @@ T = 2048
 S = 512
 HALF = 256
 BLK = 128
-LOG_ORDER = ((0, 0), (0, 1), (1, 0), (0, 2), (1, 1), (0, 3), (1, 2), (1, 3))
+VECTOR_PLANES = (0,)
 PIECES = ((0, 256), (256, 128), (384, 128))
 FLOPS = 3 * 2 * 512 * 512 * 512
 
@@ -98,17 +97,15 @@ def tile_picked_logcosh2_none_po_kernel(
         offs_t = load_list("offs_t", offs)
         w1w_raw = load_words("w1w_raw", w1_words, "w_raw")
         load_scale_rows(nc.sync, xs_all[:], x_scales, range(4))
-        xw_all = sbt("xw_all", [P, T], I32, "big")
+        xw_all = sbt("xw_all", [P, T], I32)
         nc.sync.dma_start(xw_all[:], x_words[0].rearrange("p c r -> p (c r)").bitcast(I32))
         load_scale_rows(nc.sync, w1s_raw, w1_scales, range(4))
         n1_t = load_list("n1_t", n1)
         n2_t = load_list("n2_t", n2)
-        ident = sbt("ident", [P, P], F32)
-        make_identity(nc, ident[:])
 
         y_two = [sbt("y_two%d" % t, [P, 2 * S], F32, "y_two%d" % t) for t in range(PACK + 1)]
         nc.vector.memset(y_two[0][:, S:], 0.0)
-        w1 = (deal_words("w1w", w1w_raw), deal_scales("w1s", w1s_raw, 1, nc.gpsimd))
+        w1 = (deal_words("w1w", w1w_raw), deal_scales("w1s", w1s_raw, 1, nc.vector))
         xs = sbt("xs", [P, S], U8)
         xw = sbt("xw", [P, S], U32)
         y_ps = {}
@@ -129,20 +126,16 @@ def tile_picked_logcosh2_none_po_kernel(
 
         ab = sbt("ab", [P, PACK, 2, S], F32, "ab")
         mag = sbt("mag", [P, PACK, 2, S], F32)
-        neg_b = sbt("neg_b", [P, PACK, S], F32)
-        th = sbt("th", [P, PACK, 2, S], F32)
+        th = sbt("th", [P, PACK, 2, S], F32, "th")
         for t in range(PACK):
             nc.scalar.copy(out=y_two[t][:, :HALF], in_=y_ps[0, t][:, :HALF])
             if t == 0:
                 nc.scalar.copy(out=y_two[1][:, S : S + HALF], in_=y_ps[0, 0][:, :HALF])
-        for t in range(PACK):
             nc.scalar.copy(out=y_two[t][:, HALF:S], in_=y_ps[1, t][:, :HALF])
             if t == 0:
                 nc.vector.tensor_copy(out=y_two[1][:, S + HALF :], in_=y_two[0][:, HALF:S])
             else:
                 nc.sync.dma_start(y_two[t + 1][:, S:], y_two[t][:, :S])
-        res_t = sbt("res_t", [P, PACK, S], F32, "big")
-        nc.sync.dma_start(res_t[:], res.rearrange("(p t) s -> p t s", t=PACK))
         for t in range(PACK):
             for j, lst in enumerate((n1_t, n2_t)):
                 n = HALF if (t, j) == (PACK - 1, 1) else S
@@ -153,57 +146,34 @@ def tile_picked_logcosh2_none_po_kernel(
                         in1=y_two[t + 1][:, S + lo : S + lo + n],
                         op=ALU.subtract,
                     )
-            if t == 0:
-                nc.scalar.activation(out=mag[:, t, 0, :], in_=ab[:, t, 0, :], func=ACT.Abs)
-                nc.vector.scalar_tensor_tensor(
-                    out=mag[:, t, 1, :], in0=ab[:, t, 1, :], scalar=-1.0, in1=ab[:, t, 1, :], op0=ALU.mult, op1=ALU.max
-                )
-                nc.scalar.activation(out=th[:, t, 0, :], in_=mag[:, t, 0, :], func=ACT.Tanh)
-                nc.scalar.activation(out=th[:, t, 1, :], in_=mag[:, t, 1, :], func=ACT.Tanh)
-            elif t < PACK - 1:
-                nc.scalar.activation(out=mag[:, t, :, :], in_=ab[:, t, :, :], func=ACT.Abs)
-                nc.scalar.activation(out=th[:, t, :, :], in_=mag[:, t, :, :], func=ACT.Tanh)
-            else:
-                parts = ((0, 0, S), (1, 0, HALF), (1, HALF, S))
-                for j, lo, hi in parts:
-                    nc.scalar.activation(out=mag[:, t, j, lo:hi], in_=ab[:, t, j, lo:hi], func=ACT.Abs)
-                for j, lo, hi in parts:
-                    nc.scalar.activation(out=th[:, t, j, lo:hi], in_=mag[:, t, j, lo:hi], func=ACT.Tanh)
-        turned = (S // BLK - 1) * BLK
-        nc.vector.tensor_scalar(
-            out=neg_b[:, :, :turned], in0=mag[:, :, 1, :turned], scalar1=-1.0, scalar2=None, op0=ALU.mult
-        )
-        last_diff = sbt("last_diff", [P, PACK, BLK], F32)
-        nc.vector.tensor_tensor(out=last_diff[:], in0=mag[:, :, 0, turned:], in1=mag[:, :, 1, turned:], op=ALU.subtract)
-
-        g_ps = bank(0, "g_ps")
-        for t in range(PACK):
-            nc.tensor.transpose(g_ps[:, t * P : (t + 1) * P], gain[:, t : t + 1].to_broadcast([P, P]), ident[:])
-        gains = sbt("gains", [P, S + PACK * HALF], F32, "ab")
-        gain_free = gains[:, :S].rearrange("s (u p e) -> s u p e", u=2, e=2)
-        nc.vector.tensor_copy(out=gain_free, in_=g_ps[:].rearrange("s (u e p) -> s u p e", u=2, e=2))
-        w2w = deal_words("w2w", w2w_raw, "y_two4")
-        w23s = deal_scales("w23s", ws_raw[:], 2, nc.vector, "y_two3")
-        w2 = (w2w, w23s[:, :S])
-
-        blocks = S // BLK
-        logs = {}
-        for j, k in LOG_ORDER:
-            logs[j, k] = sbt("log%d_%d" % (j, k), [P, PACK, BLK], F32, "log%d_%d" % (j, k))
-            nc.scalar.activation(out=logs[j, k][:], in_=th[:, :, j, k * BLK : (k + 1) * BLK], func=ACT.Ln, bias=1.0)
+            parts = ((0, 0, S), (1, 0, S)) if t < PACK - 1 else ((0, 0, S), (1, 0, HALF), (1, HALF, S))
+            for j, lo, hi in parts:
+                nc.scalar.activation(out=mag[:, t, j, lo:hi], in_=ab[:, t, j, lo:hi], func=ACT.Abs)
+            for j, lo, hi in parts:
+                nc.scalar.activation(out=th[:, t, j, lo:hi], in_=mag[:, t, j, lo:hi], func=ACT.Tanh)
+        w2 = (deal_words("w2w", w2w_raw, "y_two4"), deal_scales("w2s", w2s_raw, 1, nc.vector, "y_two3"))
+        res_t = sbt("res_t", [P, PACK, S], F32, "y_two2")
+        nc.sync.dma_start(res_t[:], res.rearrange("(p t) s -> p t s", t=PACK))
         w3w_raw = load_words("w3w_raw", w3_words, "w_raw")
 
-        sums = [bank(4 + k, "sums%d" % k) for k in range(blocks - 1)]
-
-        def add_turned(k, t, src, start=False, stop=False):
-            nc.tensor.matmul(sums[k][:, t * P : (t + 1) * P], src, ident[:], start=start, stop=stop, is_transpose=True)
-
-        for t in range(PACK):
-            for k in range(blocks - 1):
-                add_turned(k, t, mag[:, t, 0, k * BLK : (k + 1) * BLK], start=(t == 0))
-        for k in range(blocks - 1):
-            for t in range(PACK):
-                add_turned(k, t, neg_b[:, t, k * BLK : (k + 1) * BLK])
+        part = []
+        for h in range(2):
+            tok = slice(h * HALF, (h + 1) * HALF)
+            diff = sbt("diff%d" % h, [P, PACK, HALF], F32)
+            nc.vector.tensor_tensor(out=diff[:], in0=mag[:, :, 0, tok], in1=mag[:, :, 1, tok], op=ALU.subtract)
+            log_a = sbt("log_a%d" % h, [P, PACK, HALF], F32)
+            nc.scalar.activation(out=log_a[:], in_=th[:, :, 0, tok], func=ACT.Ln, bias=1.0)
+            part.append((diff, log_a))
+        log_b = []
+        for k, (lo, n) in enumerate(PIECES):
+            lg = sbt("log_b%d" % k, [P, PACK, n], F32)
+            nc.scalar.activation(out=lg[:], in_=th[:, :, 1, lo : lo + n], func=ACT.Ln, bias=1.0)
+            log_b.append(lg)
+        less_a = sbt("less_a", [P, PACK, S], F32)
+        for h in range(2):
+            nc.vector.tensor_tensor(
+                out=less_a[:, :, h * HALF : (h + 1) * HALF], in0=part[h][0][:], in1=part[h][1][:], op=ALU.subtract
+            )
 
         def woven(ap):
             return ap.rearrange("p (c i t) -> p c t i", i=4, t=PACK)
@@ -217,69 +187,51 @@ def tile_picked_logcosh2_none_po_kernel(
             return tiles, [tiles[t // per][:, (t % per) * n : (t % per + 1) * n] for t in range(PACK)]
 
         h_win = [sbt("h_win%d" % t, [P, S], F32) for t in range(PACK)]
-        z_turned, z_woven = {}, {}
-
-        def take_log_a(k):
-            neg = sbt("neg_log%d" % k, [P, PACK, BLK], F32)
-            nc.vector.tensor_scalar(out=neg[:], in0=logs[0, k][:], scalar1=-1.0, scalar2=None, op0=ALU.mult)
-            for t in range(PACK):
-                add_turned(k, t, neg[:, t, :])
+        sums, z_woven, h_ps = {}, {}, {}
 
         def close_sum(k):
-            for t in range(PACK):
-                add_turned(k, t, logs[1, k][:, t, :], stop=(t == PACK - 1))
-            z_turned[k] = sbt("z_turned%d" % k, [P, 2, P, 2], BF16)
-            nc.vector.tensor_tensor(
-                out=z_turned[k][:], in0=sums[k][:].rearrange("s (u e p) -> s u p e", u=2, e=2), in1=gain_free, op=ALU.mult
-            )
+            lo, n = PIECES[k]
+            sums[k] = sbt("sum%d" % k, [P, PACK, n], F32)
+            nc.vector.tensor_tensor(out=sums[k][:], in0=less_a[:, :, lo : lo + n], in1=log_b[k][:], op=ALU.add)
 
-        def turn_back(k):
-            pairs = z_turned[k][:].rearrange("s u p e -> s (u p e)").bitcast(F32)
-            back = bank(k, "back%d" % k)
-            for u in range(2):
-                nc.tensor.transpose(back[:, u * P : (u + 1) * P], pairs[:, u * P : (u + 1) * P], ident[:])
-            z_woven[k] = sbt("z%d" % k, [P, BLK * PACK], BF16)
-            nc.vector.tensor_copy(
-                out=z_woven[k][:].bitcast(F32).rearrange("p (s u) -> p s u", u=2),
-                in_=back[:, : 2 * P].rearrange("p (u s) -> p s u", u=2),
-            )
+        def weave(k):
+            lo, n = PIECES[k]
+            z_woven[k] = sbt("z%d" % k, [P, n * PACK], BF16, "z%d" % k)
+            gain_b = gain[:].unsqueeze(1).unsqueeze(3).broadcast_to([P, n // 4, PACK, 4])
+            nc.vector.tensor_tensor(out=woven(z_woven[k][:]), in0=planes(sums[k][:]), in1=gain_b, op=ALU.mult)
 
         def second_product(k):
-            zc = sbt("zc%d" % k, [P, BLK], U32)
-            zs = sbt("zs%d" % k, [P, BLK], U8)
+            lo, n = PIECES[k]
+            zc = sbt("zc%d" % k, [P, n], U32, "zc%d" % k)
+            zs = sbt("zs%d" % k, [P, n], U8)
             nc.vector.quantize_mx(out=zc[:].bitcast(FP8X4), scales=zs[:], in_=z_woven[k][:])
-            tiles, outs = banks_for(4 + k, BLK, "h_ps%d" % k)
+            if k < len(PIECES) - 1:
+                tiles, h_ps[k] = banks_for(lo // BLK, n, "h_ps%d" % k)
+            else:
+                tiles = [bank(3, "h_last0"), bank(7, "h_last1")]
+                h_ps[k] = [tiles[t // 2][:, (t % 2) * n : (t % 2 + 1) * n] for t in range(PACK)]
             for t in range(PACK):
-                product(outs[t], w2, t, zc[:], zs[:])
-            for t in range(PACK):
-                nc.scalar.activation(out=h_win[t][:, k * BLK : (k + 1) * BLK], in_=outs[t], func=ACT.Tanh)
+                product(h_ps[k][t], w2, t, zc[:], zs[:])
 
-        last = blocks - 1
-        last_part = sbt("last_part", [P, PACK, BLK], F32)
-        last_sum = sbt("last_sum", [P, PACK, BLK], F32)
-
-        def last_log_a(k):
-            nc.vector.tensor_tensor(out=last_part[:], in0=last_diff[:], in1=logs[0, k][:], op=ALU.subtract)
-
-        def last_close(k):
-            nc.vector.tensor_tensor(out=last_sum[:], in0=last_part[:], in1=logs[1, k][:], op=ALU.add)
-
-        def last_weave(k):
-            z_woven[k] = sbt("z%d" % k, [P, BLK * PACK], BF16)
-            gain_b = gain[:].unsqueeze(1).unsqueeze(3).broadcast_to([P, BLK // 4, PACK, 4])
-            nc.vector.tensor_tensor(out=woven(z_woven[k][:]), in0=planes(last_sum[:]), in1=gain_b, op=ALU.mult)
-
-        stages = (take_log_a, close_sum, turn_back, second_product)
-        last_stages = (last_log_a, last_close, last_weave, second_product)
-        for step in range(blocks + len(stages) - 1):
+        stages = (close_sum, weave, second_product)
+        for step in range(len(PIECES) + len(stages) - 1):
             for i in range(len(stages)):
-                k = step - i
-                if 0 <= k < blocks:
-                    (last_stages if k == last else stages)[i](k)
+                if 0 <= step - i < len(PIECES):
+                    stages[i](step - i)
+        warm = sbt("warm", [P, 1], F32)
+        nc.scalar.activation(out=warm[:], in_=log_b[-1][:, 0, 0:1], func=ACT.Sigmoid)
+        for t in range(PACK):
+            for k, (lo, n) in enumerate(PIECES):
+                if t in VECTOR_PLANES:
+                    nc.scalar.activation(out=h_win[t][:, lo : lo + n], in_=h_ps[k][t], func=ACT.Sigmoid, scale=2.0)
+                elif k == len(PIECES) - 1 and t >= 2:
+                    nc.vector.tensor_copy(out=h_win[t][:, lo : lo + n], in_=h_ps[k][t])
+                else:
+                    nc.scalar.copy(out=h_win[t][:, lo : lo + n], in_=h_ps[k][t])
 
-        gain_rows = gains[:, S:].rearrange("p (t s) -> p t s", t=PACK)
-        nc.vector.tensor_copy(out=gain_rows, in_=gain[:].unsqueeze(2).broadcast_to([P, PACK, HALF]))
-        w3 = (deal_words("w3w", w3w_raw, "log1_1"), w23s[:, S:])
+        gain2 = sbt("gain2", [P, PACK], F32)
+        nc.vector.tensor_scalar(out=gain2[:], in0=gain[:], scalar1=2.0, scalar2=None, op0=ALU.mult)
+        w3 = (deal_words("w3w", w3w_raw, "z2"), deal_scales("w3s", w3s_raw, 1, nc.vector, "zc2"))
         out_rows = out_0.rearrange("(p t) s -> p t s", t=PACK)
         out_words = out_1[0].rearrange("p c r -> p (c r)").bitcast(I32)
         oc = sbt("oc", [P, S], I32)
@@ -288,15 +240,24 @@ def tile_picked_logcosh2_none_po_kernel(
             tok = slice(lo, lo + n)
             g = sbt("g%d" % k, [P, PACK, n], F32)
             for t in range(PACK):
-                nc.vector.tensor_tensor(
-                    out=g[:, t, :], in0=h_win[t][:].indirect(cols(mv_t, lo, n)), in1=gain_rows[:, t, :n], op=ALU.mult
-                )
+                window = h_win[t][:].indirect(cols(mv_t, lo, n))
+                if t in VECTOR_PLANES:
+                    nc.vector.tensor_copy(out=g[:, t, :], in_=window)
+                else:
+                    nc.scalar.activation(out=g[:, t, :], in_=window, func=ACT.Sigmoid, scale=2.0)
             z2 = sbt("z2_%d" % k, [P, n * PACK], BF16, "z2_%d" % k)
-            nc.scalar.copy(out=woven(z2[:]), in_=planes(g[:]))
+            nc.vector.scalar_tensor_tensor(
+                out=z2[:].rearrange("p (s t) -> p s t", t=PACK),
+                in0=g[:].rearrange("p t s -> p s t"),
+                scalar=-0.5,
+                in1=gain2[:].unsqueeze(1).broadcast_to([P, n, PACK]),
+                op0=ALU.add,
+                op1=ALU.mult,
+            )
             z2c = sbt("z2c%d" % k, [P, n], U32)
             z2s = sbt("z2s%d" % k, [P, n], U8)
             nc.vector.quantize_mx(out=z2c[:].bitcast(FP8X4), scales=z2s[:], in_=z2[:])
-            tiles, outs = banks_for(lo // BLK, n, "o_ps%d" % k)
+            tiles, outs = banks_for(4 + lo // BLK, n, "o_ps%d" % k)
             for t in range(PACK):
                 product(outs[t], w3, t, z2c[:], z2s[:])
             o = sbt("o%d" % k, [P, PACK, n], F32)

@@ -88,24 +88,22 @@ def tile_picked_logcosh2_none_po_kernel(
         def cols(lst, start, n):
             return lst[:, start // 16 : (start + n) // 16]
 
-        xs_all = sbt("xs_all", [P, T], U8)
+        xs_all = sbt("xs_all", [P, T], U8, "xs_all")
         nc.vector.memset(xs_all[:, : 3 * T // 4].bitcast(I32), 0)
         nc.gpsimd.memset(xs_all[:, 3 * T // 4 :].bitcast(I32), 0)
-        w1s_raw = zeroed("w1s_raw", S, nc.gpsimd, "w1s_raw")[:]
-        ws_raw = zeroed("ws_raw", 2 * S, nc.vector)
-        w2s_raw, w3s_raw = (ws_raw[:, i * S : (i + 1) * S] for i in range(2))
+        ws_raw = zeroed("ws_raw", S, nc.gpsimd)[:]
         offs_t = load_list("offs_t", offs)
-        w1w_raw = load_words("w1w_raw", w1_words, "w_raw")
+        w1w_raw = load_words("w1w_raw", w1_words, "ab")
         load_scale_rows(nc.sync, xs_all[:], x_scales, range(4))
         xw_all = sbt("xw_all", [P, T], I32)
         nc.sync.dma_start(xw_all[:], x_words[0].rearrange("p c r -> p (c r)").bitcast(I32))
-        load_scale_rows(nc.sync, w1s_raw, w1_scales, range(4))
+        load_scale_rows(nc.sync, ws_raw, w1_scales, range(4))
         n1_t = load_list("n1_t", n1)
         n2_t = load_list("n2_t", n2)
 
         y_two = [sbt("y_two%d" % t, [P, 2 * S], F32, "y_two%d" % t) for t in range(PACK + 1)]
         nc.vector.memset(y_two[0][:, S:], 0.0)
-        w1 = (deal_words("w1w", w1w_raw), deal_scales("w1s", w1s_raw, 1, nc.vector))
+        w1 = (deal_words("w1w", w1w_raw), deal_scales("w1s", ws_raw, 1, nc.vector))
         xs = sbt("xs", [P, S], U8)
         xw = sbt("xw", [P, S], U32)
         y_ps = {}
@@ -117,23 +115,22 @@ def tile_picked_logcosh2_none_po_kernel(
                 y_ps[h, t] = bank(4 * h + t, "y_ps%d_%d" % (h, t))
                 product(y_ps[h, t][:, :HALF], w1, t, xw[:, tok], xs[:, tok])
 
-        w2w_raw = load_words("w2w_raw", w2_words, "w_raw")
-        gain = sbt("gain", [P, PACK], F32, "w1s_raw")
-        nc.sync.dma_start(gain[:], gn.rearrange("(p t) o -> p (t o)", t=PACK))
-        load_scale_rows(nc.sync, w2s_raw, w2_scales, range(4))
-        load_scale_rows(nc.sync, w3s_raw, w3_scales, range(4))
+        w2w = deal_words("w2w", load_words("w2w_raw", w2_words, "ab"))
         mv_t = load_list("mv_t", mv)
+        load_scale_rows(nc.sync, ws_raw, w2_scales, range(4))
+        gain = sbt("gain", [P, PACK], F32, "xs_all")
+        nc.sync.dma_start(gain[:], gn.rearrange("(p t) o -> p (t o)", t=PACK))
 
         ab = sbt("ab", [P, PACK, 2, S], F32, "ab")
         mag = sbt("mag", [P, PACK, 2, S], F32)
         th = sbt("th", [P, PACK, 2, S], F32, "th")
         for t in range(PACK):
             nc.scalar.copy(out=y_two[t][:, :HALF], in_=y_ps[0, t][:, :HALF])
-            if t == 0:
-                nc.scalar.copy(out=y_two[1][:, S : S + HALF], in_=y_ps[0, 0][:, :HALF])
+            if t < 2:
+                nc.scalar.copy(out=y_two[t + 1][:, S : S + HALF], in_=y_ps[0, t][:, :HALF])
             nc.scalar.copy(out=y_two[t][:, HALF:S], in_=y_ps[1, t][:, :HALF])
-            if t == 0:
-                nc.vector.tensor_copy(out=y_two[1][:, S + HALF :], in_=y_two[0][:, HALF:S])
+            if t < 2:
+                nc.vector.tensor_copy(out=y_two[t + 1][:, S + HALF :], in_=y_two[t][:, HALF:S])
             else:
                 nc.sync.dma_start(y_two[t + 1][:, S:], y_two[t][:, :S])
         for t in range(PACK):
@@ -151,29 +148,29 @@ def tile_picked_logcosh2_none_po_kernel(
                 nc.scalar.activation(out=mag[:, t, j, lo:hi], in_=ab[:, t, j, lo:hi], func=ACT.Abs)
             for j, lo, hi in parts:
                 nc.scalar.activation(out=th[:, t, j, lo:hi], in_=mag[:, t, j, lo:hi], func=ACT.Tanh)
-        w2 = (deal_words("w2w", w2w_raw, "y_two4"), deal_scales("w2s", w2s_raw, 1, nc.vector, "y_two3"))
+        w2 = (w2w, deal_scales("w2s", ws_raw, 1, nc.vector, "y_two3"))
+        load_scale_rows(nc.sync, ws_raw, w3_scales, range(4))
         res_t = sbt("res_t", [P, PACK, S], F32, "y_two2")
         nc.sync.dma_start(res_t[:], res.rearrange("(p t) s -> p t s", t=PACK))
-        w3w_raw = load_words("w3w_raw", w3_words, "w_raw")
+        w3w_raw = load_words("w3w_raw", w3_words, "y_two1")
 
-        part = []
-        for h in range(2):
-            tok = slice(h * HALF, (h + 1) * HALF)
-            diff = sbt("diff%d" % h, [P, PACK, HALF], F32)
-            nc.vector.tensor_tensor(out=diff[:], in0=mag[:, :, 0, tok], in1=mag[:, :, 1, tok], op=ALU.subtract)
-            log_a = sbt("log_a%d" % h, [P, PACK, HALF], F32)
-            nc.scalar.activation(out=log_a[:], in_=th[:, :, 0, tok], func=ACT.Ln, bias=1.0)
-            part.append((diff, log_a))
-        log_b = []
-        for k, (lo, n) in enumerate(PIECES):
-            lg = sbt("log_b%d" % k, [P, PACK, n], F32)
-            nc.scalar.activation(out=lg[:], in_=th[:, :, 1, lo : lo + n], func=ACT.Ln, bias=1.0)
-            log_b.append(lg)
+        diff = sbt("diff", [P, PACK, S], F32)
+        for lo in range(0, S, HALF):
+            tok = slice(lo, lo + HALF)
+            nc.vector.tensor_tensor(out=diff[:, :, tok], in0=mag[:, :, 0, tok], in1=mag[:, :, 1, tok], op=ALU.subtract)
+        logs = {}
+        for j, lo, n in ((0, 0, BLK), (0, BLK, BLK), (1, 0, HALF), (0, HALF, HALF), (1, HALF, BLK), (1, HALF + BLK, BLK)):
+            logs[j, lo] = sbt("log%d_%d" % (j, lo), [P, PACK, n], F32)
+            nc.scalar.activation(out=logs[j, lo][:], in_=th[:, :, j, lo : lo + n], func=ACT.Ln, bias=1.0)
+        log_b = [logs[1, lo] for lo, n in PIECES]
         less_a = sbt("less_a", [P, PACK, S], F32)
-        for h in range(2):
-            nc.vector.tensor_tensor(
-                out=less_a[:, :, h * HALF : (h + 1) * HALF], in0=part[h][0][:], in1=part[h][1][:], op=ALU.subtract
-            )
+
+        def take_log_a(lo, n):
+            tok = slice(lo, lo + n)
+            nc.vector.tensor_tensor(out=less_a[:, :, tok], in0=diff[:, :, tok], in1=logs[0, lo][:], op=ALU.subtract)
+
+        take_log_a(0, BLK)
+        take_log_a(BLK, BLK)
 
         def woven(ap):
             return ap.rearrange("p (c i t) -> p c t i", i=4, t=PACK)
@@ -218,6 +215,8 @@ def tile_picked_logcosh2_none_po_kernel(
             for i in range(len(stages)):
                 if 0 <= step - i < len(PIECES):
                     stages[i](step - i)
+            if step == 0:
+                take_log_a(HALF, HALF)
         warm = sbt("warm", [P, 1], F32)
         nc.scalar.activation(out=warm[:], in_=log_b[-1][:, 0, 0:1], func=ACT.Sigmoid)
         for t in range(PACK):
@@ -231,49 +230,70 @@ def tile_picked_logcosh2_none_po_kernel(
 
         gain2 = sbt("gain2", [P, PACK], F32)
         nc.vector.tensor_scalar(out=gain2[:], in0=gain[:], scalar1=2.0, scalar2=None, op0=ALU.mult)
-        w3 = (deal_words("w3w", w3w_raw, "z2"), deal_scales("w3s", w3s_raw, 1, nc.vector, "zc2"))
+        w3 = (deal_words("w3w", w3w_raw, "z2"), deal_scales("w3s", ws_raw, 1, nc.vector))
         out_rows = out_0.rearrange("(p t) s -> p t s", t=PACK)
         out_words = out_1[0].rearrange("p c r -> p (c r)").bitcast(I32)
         oc = sbt("oc", [P, S], I32)
         osc = sbt("osc", [P, S], U8)
+        fetched, z2, o_ps, o_sb, o_woven = {}, {}, {}, {}, {}
         for k, (lo, n) in enumerate(PIECES):
-            tok = slice(lo, lo + n)
-            g = sbt("g%d" % k, [P, PACK, n], F32)
+            fetched[k] = sbt("fetched%d" % k, [P, PACK, n], F32)
             for t in range(PACK):
                 window = h_win[t][:].indirect(cols(mv_t, lo, n))
                 if t in VECTOR_PLANES:
-                    nc.vector.tensor_copy(out=g[:, t, :], in_=window)
+                    nc.vector.tensor_copy(out=fetched[k][:, t, :], in_=window)
                 else:
-                    nc.scalar.activation(out=g[:, t, :], in_=window, func=ACT.Sigmoid, scale=2.0)
-            z2 = sbt("z2_%d" % k, [P, n * PACK], BF16, "z2_%d" % k)
+                    nc.scalar.activation(out=fetched[k][:, t, :], in_=window, func=ACT.Sigmoid, scale=2.0)
+
+        def weave2(k):
+            lo, n = PIECES[k]
+            z2[k] = sbt("z2_%d" % k, [P, n * PACK], BF16)
             nc.vector.scalar_tensor_tensor(
-                out=z2[:].rearrange("p (s t) -> p s t", t=PACK),
-                in0=g[:].rearrange("p t s -> p s t"),
+                out=z2[k][:].rearrange("p (s t) -> p s t", t=PACK),
+                in0=fetched[k][:].rearrange("p t s -> p s t"),
                 scalar=-0.5,
                 in1=gain2[:].unsqueeze(1).broadcast_to([P, n, PACK]),
                 op0=ALU.add,
                 op1=ALU.mult,
             )
+
+        def third_product(k):
+            lo, n = PIECES[k]
             z2c = sbt("z2c%d" % k, [P, n], U32)
             z2s = sbt("z2s%d" % k, [P, n], U8)
-            nc.vector.quantize_mx(out=z2c[:].bitcast(FP8X4), scales=z2s[:], in_=z2[:])
-            tiles, outs = banks_for(4 + lo // BLK, n, "o_ps%d" % k)
+            nc.vector.quantize_mx(out=z2c[:].bitcast(FP8X4), scales=z2s[:], in_=z2[k][:])
+            o_ps[k], outs = banks_for(4 + lo // BLK, n, "o_ps%d" % k)
             for t in range(PACK):
                 product(outs[t], w3, t, z2c[:], z2s[:])
-            o = sbt("o%d" % k, [P, PACK, n], F32)
+
+        for step in range(len(PIECES) + 1):
+            if step < len(PIECES):
+                weave2(step)
+            if step > 0:
+                third_product(step - 1)
+
+        for k, (lo, n) in enumerate(PIECES):
+            tok = slice(lo, lo + n)
+            o_sb[k] = sbt("o%d" % k, [P, PACK, n], F32)
             per = 512 // n
-            for i, tile in enumerate(tiles):
+            for i, tile in enumerate(o_ps[k]):
                 rows = slice(i * per, (i + 1) * per)
                 nc.vector.tensor_tensor(
-                    out=o[:, rows, :], in0=tile[:].rearrange("p (t s) -> p t s", t=per), in1=res_t[:, rows, tok], op=ALU.add
+                    out=o_sb[k][:, rows, :],
+                    in0=tile[:].rearrange("p (t s) -> p t s", t=per),
+                    in1=res_t[:, rows, tok],
+                    op=ALU.add,
                 )
-            nc.sync.dma_start(out_rows[:, :, tok], o[:])
-            ob = sbt("ob%d" % k, [P, n * PACK], BF16)
-            if k == 2:
-                nc.vector.tensor_copy(out=woven(ob[:]), in_=planes(o[:]))
+            nc.sync.dma_start(out_rows[:, :, tok], o_sb[k][:])
+        for k, (lo, n) in enumerate(PIECES):
+            o_woven[k] = sbt("ob%d" % k, [P, n * PACK], BF16)
+            if k == len(PIECES) - 1:
+                nc.vector.tensor_copy(out=woven(o_woven[k][:]), in_=planes(o_sb[k][:]))
             else:
-                nc.scalar.copy(out=woven(ob[:]), in_=planes(o[:]))
-            nc.vector.quantize_mx(out=oc[:, tok].bitcast(FP8X4), scales=osc[:, tok], in_=ob[:])
-            nc.sync.dma_start(out_words[:, tok], oc[:, tok])
+                nc.scalar.copy(out=woven(o_woven[k][:]), in_=planes(o_sb[k][:]))
+        for k, (lo, n) in enumerate(PIECES):
+            tok = slice(lo, lo + n)
+            nc.vector.quantize_mx(out=oc[:, tok].bitcast(FP8X4), scales=osc[:, tok], in_=o_woven[k][:])
+        nc.sync.dma_start(out_words, oc[:])
         for q in range(4):
             (nc.sync if q % 2 else nc.scalar).dma_start(out_2[0, 4 * q : 4 * q + 4, :].bitcast(I32), osc[32 * q : 32 * q + 4, :].bitcast(I32))

@@ -17,10 +17,15 @@ P = 128
 PACK = 4
 T = 2048
 S = 512
-HALF = 256
-BLK = 128
-VECTOR_PLANES = (0,)
-PIECES = ((0, 256), (256, 128), (384, 128))
+HALF = S // 2
+QUARTER = S // 4
+BANK = 512
+QUADRANTS = 4
+PIECES = ((0, HALF), (HALF, QUARTER), (HALF + QUARTER, QUARTER))
+LAST = len(PIECES) - 1
+VECTOR_PLANE = 0
+ZEROED_BY_VECTOR = 3 * T // 4
+ENGINE_COPIES = 2
 FLOPS = 3 * 2 * 512 * 512 * 512
 
 
@@ -37,119 +42,127 @@ def tile_picked_logcosh2_none_po_kernel(
             return sb.tile(shape, dtype, name=name, tag=tag, align_bytes=64)
 
         def bank(i, name):
-            return ps.tile([P, 512], F32, name=name, tag="bank%d" % i)
+            return ps.tile([P, BANK], F32, name=name, tag="bank%d" % i)
 
         def load_list(name, src):
             tile = sb.tile([P, S // 16], U16, name=name)
             nc.sync.dma_start(tile[:], src)
             return tile
 
-        def load_scale_rows(queue, tile, src, quadrants):
-            for q in quadrants:
-                queue.dma_start(tile[32 * q : 32 * q + 4, :].bitcast(I32), src[0, 4 * q : 4 * q + 4, :].bitcast(I32))
+        def load_scale_rows(tile, src):
+            for q in range(QUADRANTS):
+                nc.sync.dma_start(tile[32 * q : 32 * q + 4, :].bitcast(I32), src[0, 4 * q : 4 * q + 4, :].bitcast(I32))
 
-        def zeroed(name, width, engine, tag=""):
-            tile = sbt(name, [P, width], U8, tag)
-            engine.memset(tile[:].bitcast(I32), 0)
-            return tile
-
-        def deal_words(name, raw_words, tag=""):
-            words = sbt(name, [P, PACK * P * 2], U8, tag)
-            nc.vector.tensor_copy(
-                out=words[:].rearrange("p (t c i b) -> p c t i b", t=PACK, i=8, b=2),
-                in_=raw_words[:].rearrange("p (c i t b) -> p c t i b", t=PACK, i=8, b=2),
-            )
-            return words
-
-        def deal_scales(name, raw_scales, n, engine, tag=""):
-            scales = sbt(name, [P, n * S], U8, tag)
-            engine.tensor_copy(
-                out=scales[:].rearrange("p (w t m) -> p w t m", w=n, t=PACK),
-                in_=raw_scales.rearrange("p (w m t) -> p w t m", w=n, t=PACK),
-            )
-            return scales
-
-        def load_words(name, src, tag=""):
-            tile = sb.tile([P, 1024], U8, name=name, tag=tag, align_bytes=64)
+        def load_words(name, src, tag):
+            tile = sbt(name, [P, 2 * S], U8, tag)
             nc.sync.dma_start(tile[:].bitcast(I32), src[0].bitcast(I32))
             return tile
 
-        def product(out, w, t, codes, scales):
+        def deal_words(name, raw, tag=""):
+            words = sbt(name, [P, 2 * S], U8, tag)
+            nc.vector.tensor_copy(
+                out=words[:].rearrange("p (t c i b) -> p c t i b", t=PACK, i=8, b=2),
+                in_=raw[:].rearrange("p (c i t b) -> p c t i b", t=PACK, i=8, b=2),
+            )
+            return words
+
+        def deal_scales(name, raw, tag=""):
+            scales = sbt(name, [P, S], U8, tag)
+            nc.vector.tensor_copy(
+                out=scales[:].rearrange("p (t m) -> p t m", t=PACK), in_=raw[:].rearrange("p (m t) -> p t m", t=PACK)
+            )
+            return scales
+
+        def product(out, weight, t, codes, scales):
+            words, weight_scales = weight
             nc.tensor.matmul_mx(
                 out=out,
-                lhsT=w[0][:, 2 * P * t : 2 * P * (t + 1)].bitcast(FP4X4),
-                lhsT_scale=w[1][:, P * t : P * (t + 1)],
+                lhsT=words[:, 2 * P * t : 2 * P * (t + 1)].bitcast(FP4X4),
+                lhsT_scale=weight_scales[:, P * t : P * (t + 1)],
                 rhs=codes.bitcast(FP8X4),
                 rhs_scale=scales,
                 start=True,
                 stop=True,
             )
 
-        def cols(lst, start, n):
-            return lst[:, start // 16 : (start + n) // 16]
+        def entries(lst, lo, n):
+            return lst[:, lo // 16 : (lo + n) // 16]
+
+        def plane_slots(banks, n):
+            per = PACK // len(banks)
+            return [banks[t // per][:, (t % per) * n : (t % per + 1) * n] for t in range(PACK)]
+
+        def woven(ap):
+            return ap.rearrange("p (c i t) -> p c t i", i=4, t=PACK)
+
+        def planes(ap):
+            return ap.rearrange("p t (c i) -> p c t i", i=4)
 
         xs_all = sbt("xs_all", [P, T], U8, "xs_all")
-        nc.vector.memset(xs_all[:, : 3 * T // 4].bitcast(I32), 0)
-        nc.gpsimd.memset(xs_all[:, 3 * T // 4 :].bitcast(I32), 0)
-        ws_raw = zeroed("ws_raw", S, nc.gpsimd)[:]
+        nc.vector.memset(xs_all[:, :ZEROED_BY_VECTOR].bitcast(I32), 0)
+        nc.gpsimd.memset(xs_all[:, ZEROED_BY_VECTOR:].bitcast(I32), 0)
+        ws_raw = sbt("ws_raw", [P, S], U8)
+        nc.gpsimd.memset(ws_raw[:].bitcast(I32), 0)
         offs_t = load_list("offs_t", offs)
         w1w_raw = load_words("w1w_raw", w1_words, "ab")
-        load_scale_rows(nc.sync, xs_all[:], x_scales, range(4))
+        load_scale_rows(xs_all, x_scales)
         xw_all = sbt("xw_all", [P, T], I32)
         nc.sync.dma_start(xw_all[:], x_words[0].rearrange("p c r -> p (c r)").bitcast(I32))
-        load_scale_rows(nc.sync, ws_raw, w1_scales, range(4))
+        load_scale_rows(ws_raw, w1_scales)
         n1_t = load_list("n1_t", n1)
         n2_t = load_list("n2_t", n2)
 
-        y_two = [sbt("y_two%d" % t, [P, 2 * S], F32, "y_two%d" % t) for t in range(PACK + 1)]
+        y_two = [sbt("y_two%d" % t, [P, 2 * S], F32, "y_two%d" % t) for t in range(PACK)]
+        y_last = sbt("y_last", [P, S], F32)
+        y_own = [y_two[t + 1][:, S:] for t in range(PACK - 1)] + [y_last[:]]
         nc.vector.memset(y_two[0][:, S:], 0.0)
-        w1 = (deal_words("w1w", w1w_raw), deal_scales("w1s", ws_raw, 1, nc.vector))
+        w1 = (deal_words("w1w", w1w_raw), deal_scales("w1s", ws_raw))
         xs = sbt("xs", [P, S], U8)
         xw = sbt("xw", [P, S], U32)
         y_ps = {}
-        for h in range(2):
-            tok = slice(h * HALF, (h + 1) * HALF)
-            nc.vector.tensor_copy(out=xs[:, tok], in_=xs_all[:].indirect(cols(offs_t, h * HALF, HALF)))
-            nc.vector.tensor_copy(out=xw[:, tok], in_=xw_all[:].bitcast(U32).indirect(cols(offs_t, h * HALF, HALF)))
+        for half in range(2):
+            tok = slice(half * HALF, (half + 1) * HALF)
+            picked = entries(offs_t, half * HALF, HALF)
+            nc.vector.tensor_copy(out=xs[:, tok], in_=xs_all[:].indirect(picked))
+            nc.vector.tensor_copy(out=xw[:, tok], in_=xw_all[:].bitcast(U32).indirect(picked))
             for t in range(PACK):
-                y_ps[h, t] = bank(4 * h + t, "y_ps%d_%d" % (h, t))
-                product(y_ps[h, t][:, :HALF], w1, t, xw[:, tok], xs[:, tok])
+                y_ps[half, t] = bank(PACK * half + t, "y_ps%d_%d" % (half, t))
+                product(y_ps[half, t][:, :HALF], w1, t, xw[:, tok], xs[:, tok])
 
         w2w = deal_words("w2w", load_words("w2w_raw", w2_words, "ab"))
         mv_t = load_list("mv_t", mv)
-        load_scale_rows(nc.sync, ws_raw, w2_scales, range(4))
+        load_scale_rows(ws_raw, w2_scales)
         gain = sbt("gain", [P, PACK], F32, "xs_all")
         nc.sync.dma_start(gain[:], gn.rearrange("(p t) o -> p (t o)", t=PACK))
 
         ab = sbt("ab", [P, PACK, 2, S], F32, "ab")
         mag = sbt("mag", [P, PACK, 2, S], F32)
-        th = sbt("th", [P, PACK, 2, S], F32, "th")
+        th = sbt("th", [P, PACK, 2, S], F32)
         for t in range(PACK):
             nc.scalar.copy(out=y_two[t][:, :HALF], in_=y_ps[0, t][:, :HALF])
-            if t < 2:
-                nc.scalar.copy(out=y_two[t + 1][:, S : S + HALF], in_=y_ps[0, t][:, :HALF])
+            if t < ENGINE_COPIES:
+                nc.scalar.copy(out=y_own[t][:, :HALF], in_=y_ps[0, t][:, :HALF])
             nc.scalar.copy(out=y_two[t][:, HALF:S], in_=y_ps[1, t][:, :HALF])
-            if t < 2:
-                nc.vector.tensor_copy(out=y_two[t + 1][:, S + HALF :], in_=y_two[t][:, HALF:S])
+            if t < ENGINE_COPIES:
+                nc.vector.tensor_copy(out=y_own[t][:, HALF:], in_=y_two[t][:, HALF:S])
             else:
-                nc.sync.dma_start(y_two[t + 1][:, S:], y_two[t][:, :S])
+                nc.sync.dma_start(y_own[t], y_two[t][:, :S])
         for t in range(PACK):
-            for j, lst in enumerate((n1_t, n2_t)):
-                n = HALF if (t, j) == (PACK - 1, 1) else S
-                for lo in range(0, S, n):
-                    nc.vector.tensor_tensor(
-                        out=ab[:, t, j, lo : lo + n],
-                        in0=y_two[t][:].indirect(cols(lst, lo, n)),
-                        in1=y_two[t + 1][:, S + lo : S + lo + n],
-                        op=ALU.subtract,
-                    )
-            parts = ((0, 0, S), (1, 0, S)) if t < PACK - 1 else ((0, 0, S), (1, 0, HALF), (1, HALF, S))
-            for j, lo, hi in parts:
-                nc.scalar.activation(out=mag[:, t, j, lo:hi], in_=ab[:, t, j, lo:hi], func=ACT.Abs)
-            for j, lo, hi in parts:
-                nc.scalar.activation(out=th[:, t, j, lo:hi], in_=mag[:, t, j, lo:hi], func=ACT.Tanh)
-        w2 = (w2w, deal_scales("w2s", ws_raw, 1, nc.vector, "y_two3"))
-        load_scale_rows(nc.sync, ws_raw, w3_scales, range(4))
+            parts = ((0, 0, S), (1, 0, S)) if t < PACK - 1 else ((0, 0, S), (1, 0, HALF), (1, HALF, HALF))
+            for j, lo, n in parts:
+                nc.vector.tensor_tensor(
+                    out=ab[:, t, j, lo : lo + n],
+                    in0=y_two[t][:].indirect(entries((n1_t, n2_t)[j], lo, n)),
+                    in1=y_own[t][:, lo : lo + n],
+                    op=ALU.subtract,
+                )
+            for j, lo, n in parts:
+                nc.scalar.activation(out=mag[:, t, j, lo : lo + n], in_=ab[:, t, j, lo : lo + n], func=ACT.Abs)
+            for j, lo, n in parts:
+                nc.scalar.activation(out=th[:, t, j, lo : lo + n], in_=mag[:, t, j, lo : lo + n], func=ACT.Tanh)
+
+        w2 = (w2w, deal_scales("w2s", ws_raw, "y_two3"))
+        load_scale_rows(ws_raw, w3_scales)
         res_t = sbt("res_t", [P, PACK, S], F32, "y_two2")
         nc.sync.dma_start(res_t[:], res.rearrange("(p t) s -> p t s", t=PACK))
         w3w_raw = load_words("w3w_raw", w3_words, "y_two1")
@@ -159,123 +172,117 @@ def tile_picked_logcosh2_none_po_kernel(
             tok = slice(lo, lo + HALF)
             nc.vector.tensor_tensor(out=diff[:, :, tok], in0=mag[:, :, 0, tok], in1=mag[:, :, 1, tok], op=ALU.subtract)
         logs = {}
-        for j, lo, n in ((0, 0, BLK), (0, BLK, BLK), (1, 0, HALF), (0, HALF, HALF), (1, HALF, BLK), (1, HALF + BLK, BLK)):
+
+        def log_of(j, lo, n):
             logs[j, lo] = sbt("log%d_%d" % (j, lo), [P, PACK, n], F32)
             nc.scalar.activation(out=logs[j, lo][:], in_=th[:, :, j, lo : lo + n], func=ACT.Ln, bias=1.0)
-        log_b = [logs[1, lo] for lo, n in PIECES]
+
+        log_of(0, 0, QUARTER)
+        log_of(0, QUARTER, QUARTER)
+        log_of(1, *PIECES[0])
+        log_of(0, HALF, HALF)
+        log_of(1, *PIECES[1])
+        log_of(1, *PIECES[2])
         less_a = sbt("less_a", [P, PACK, S], F32)
+        h_win = [sbt("h_win%d" % t, [P, S], F32) for t in range(PACK)]
+        sums, z_woven, h_ps = {}, {}, {}
 
         def take_log_a(lo, n):
             tok = slice(lo, lo + n)
             nc.vector.tensor_tensor(out=less_a[:, :, tok], in0=diff[:, :, tok], in1=logs[0, lo][:], op=ALU.subtract)
 
-        take_log_a(0, BLK)
-        take_log_a(BLK, BLK)
-
-        def woven(ap):
-            return ap.rearrange("p (c i t) -> p c t i", i=4, t=PACK)
-
-        def planes(ap):
-            return ap.rearrange("p t (c i) -> p c t i", i=4)
-
-        def banks_for(first, n, name):
-            per = 512 // n
-            tiles = [bank(first + i, "%s_%d" % (name, i)) for i in range(PACK // per)]
-            return tiles, [tiles[t // per][:, (t % per) * n : (t % per + 1) * n] for t in range(PACK)]
-
-        h_win = [sbt("h_win%d" % t, [P, S], F32) for t in range(PACK)]
-        sums, z_woven, h_ps = {}, {}, {}
-
-        def close_sum(k):
+        def add_log_b(k):
             lo, n = PIECES[k]
             sums[k] = sbt("sum%d" % k, [P, PACK, n], F32)
-            nc.vector.tensor_tensor(out=sums[k][:], in0=less_a[:, :, lo : lo + n], in1=log_b[k][:], op=ALU.add)
+            nc.vector.tensor_tensor(out=sums[k][:], in0=less_a[:, :, lo : lo + n], in1=logs[1, lo][:], op=ALU.add)
 
-        def weave(k):
+        def weave_z(k):
             lo, n = PIECES[k]
             z_woven[k] = sbt("z%d" % k, [P, n * PACK], BF16, "z%d" % k)
-            gain_b = gain[:].unsqueeze(1).unsqueeze(3).broadcast_to([P, n // 4, PACK, 4])
-            nc.vector.tensor_tensor(out=woven(z_woven[k][:]), in0=planes(sums[k][:]), in1=gain_b, op=ALU.mult)
+            gain_rows = gain[:].unsqueeze(1).unsqueeze(3).broadcast_to([P, n // 4, PACK, 4])
+            nc.vector.tensor_tensor(out=woven(z_woven[k][:]), in0=planes(sums[k][:]), in1=gain_rows, op=ALU.mult)
+
+        h_banks = ((0, 1), (2,), (3, 7))
 
         def second_product(k):
             lo, n = PIECES[k]
-            zc = sbt("zc%d" % k, [P, n], U32, "zc%d" % k)
-            zs = sbt("zs%d" % k, [P, n], U8)
-            nc.vector.quantize_mx(out=zc[:].bitcast(FP8X4), scales=zs[:], in_=z_woven[k][:])
-            if k < len(PIECES) - 1:
-                tiles, h_ps[k] = banks_for(lo // BLK, n, "h_ps%d" % k)
-            else:
-                tiles = [bank(3, "h_last0"), bank(7, "h_last1")]
-                h_ps[k] = [tiles[t // 2][:, (t % 2) * n : (t % 2 + 1) * n] for t in range(PACK)]
+            codes = sbt("zc%d" % k, [P, n], U32)
+            scales = sbt("zs%d" % k, [P, n], U8)
+            nc.vector.quantize_mx(out=codes[:].bitcast(FP8X4), scales=scales[:], in_=z_woven[k][:])
+            h_ps[k] = plane_slots([bank(i, "h_ps%d" % i) for i in h_banks[k]], n)
             for t in range(PACK):
-                product(h_ps[k][t], w2, t, zc[:], zs[:])
+                product(h_ps[k][t], w2, t, codes[:], scales[:])
 
-        stages = (close_sum, weave, second_product)
-        for step in range(len(PIECES) + len(stages) - 1):
-            for i in range(len(stages)):
-                if 0 <= step - i < len(PIECES):
-                    stages[i](step - i)
-            if step == 0:
-                take_log_a(HALF, HALF)
-        warm = sbt("warm", [P, 1], F32)
-        nc.scalar.activation(out=warm[:], in_=log_b[-1][:, 0, 0:1], func=ACT.Sigmoid)
+        take_log_a(0, QUARTER)
+        take_log_a(QUARTER, QUARTER)
+        add_log_b(0)
+        take_log_a(HALF, HALF)
+        for k in range(len(PIECES)):
+            weave_z(k)
+            if k < LAST:
+                add_log_b(k + 1)
+            second_product(k)
+
+        half_one = sbt("half_one", [P, 1], F32)
+        nc.scalar.activation(out=half_one[:], in_=logs[1, PIECES[LAST][0]][:, 0, 0:1], func=ACT.Sigmoid, scale=0.0)
+
         for t in range(PACK):
             for k, (lo, n) in enumerate(PIECES):
-                if t in VECTOR_PLANES:
+                if t == VECTOR_PLANE:
                     nc.scalar.activation(out=h_win[t][:, lo : lo + n], in_=h_ps[k][t], func=ACT.Sigmoid, scale=2.0)
-                elif k == len(PIECES) - 1 and t >= 2:
+                elif k == LAST and t >= PACK // 2:
                     nc.vector.tensor_copy(out=h_win[t][:, lo : lo + n], in_=h_ps[k][t])
                 else:
                     nc.scalar.copy(out=h_win[t][:, lo : lo + n], in_=h_ps[k][t])
 
         gain2 = sbt("gain2", [P, PACK], F32)
         nc.vector.tensor_scalar(out=gain2[:], in0=gain[:], scalar1=2.0, scalar2=None, op0=ALU.mult)
-        w3 = (deal_words("w3w", w3w_raw, "z2"), deal_scales("w3s", ws_raw, 1, nc.vector))
-        out_rows = out_0.rearrange("(p t) s -> p t s", t=PACK)
-        out_words = out_1[0].rearrange("p c r -> p (c r)").bitcast(I32)
-        oc = sbt("oc", [P, S], I32)
-        osc = sbt("osc", [P, S], U8)
-        fetched, z2, o_ps, o_sb, o_woven = {}, {}, {}, {}, {}
+        w3 = (deal_words("w3w", w3w_raw, "z%d" % LAST), deal_scales("w3s", ws_raw))
+
+        fetched, z2_woven, o_ps, o_sb, o_woven = {}, {}, {}, {}, {}
         for k, (lo, n) in enumerate(PIECES):
             fetched[k] = sbt("fetched%d" % k, [P, PACK, n], F32)
             for t in range(PACK):
-                window = h_win[t][:].indirect(cols(mv_t, lo, n))
-                if t in VECTOR_PLANES:
+                window = h_win[t][:].indirect(entries(mv_t, lo, n))
+                if t == VECTOR_PLANE:
                     nc.vector.tensor_copy(out=fetched[k][:, t, :], in_=window)
                 else:
                     nc.scalar.activation(out=fetched[k][:, t, :], in_=window, func=ACT.Sigmoid, scale=2.0)
 
-        def weave2(k):
+        def weave_z2(k):
             lo, n = PIECES[k]
-            z2[k] = sbt("z2_%d" % k, [P, n * PACK], BF16)
+            z2_woven[k] = sbt("z2_%d" % k, [P, n * PACK], BF16)
             nc.vector.scalar_tensor_tensor(
-                out=z2[k][:].rearrange("p (s t) -> p s t", t=PACK),
+                out=z2_woven[k][:].rearrange("p (s t) -> p s t", t=PACK),
                 in0=fetched[k][:].rearrange("p t s -> p s t"),
-                scalar=-0.5,
+                scalar=half_one[:],
                 in1=gain2[:].unsqueeze(1).broadcast_to([P, n, PACK]),
-                op0=ALU.add,
+                op0=ALU.subtract,
                 op1=ALU.mult,
             )
 
+        o_banks = ((4, 5), (6,), (7,))
+
         def third_product(k):
             lo, n = PIECES[k]
-            z2c = sbt("z2c%d" % k, [P, n], U32)
-            z2s = sbt("z2s%d" % k, [P, n], U8)
-            nc.vector.quantize_mx(out=z2c[:].bitcast(FP8X4), scales=z2s[:], in_=z2[k][:])
-            o_ps[k], outs = banks_for(4 + lo // BLK, n, "o_ps%d" % k)
-            for t in range(PACK):
-                product(outs[t], w3, t, z2c[:], z2s[:])
+            codes = sbt("z2c%d" % k, [P, n], U32)
+            scales = sbt("z2s%d" % k, [P, n], U8)
+            nc.vector.quantize_mx(out=codes[:].bitcast(FP8X4), scales=scales[:], in_=z2_woven[k][:])
+            o_ps[k] = [bank(i, "o_ps%d" % i) for i in o_banks[k]]
+            for t, slot in enumerate(plane_slots(o_ps[k], n)):
+                product(slot, w3, t, codes[:], scales[:])
 
         for step in range(len(PIECES) + 1):
-            if step < len(PIECES):
-                weave2(step)
+            if step <= LAST:
+                weave_z2(step)
             if step > 0:
                 third_product(step - 1)
 
+        out_rows = out_0.rearrange("(p t) s -> p t s", t=PACK)
         for k, (lo, n) in enumerate(PIECES):
             tok = slice(lo, lo + n)
             o_sb[k] = sbt("o%d" % k, [P, PACK, n], F32)
-            per = 512 // n
+            per = BANK // n
             for i, tile in enumerate(o_ps[k]):
                 rows = slice(i * per, (i + 1) * per)
                 nc.vector.tensor_tensor(
@@ -287,13 +294,16 @@ def tile_picked_logcosh2_none_po_kernel(
             nc.sync.dma_start(out_rows[:, :, tok], o_sb[k][:])
         for k, (lo, n) in enumerate(PIECES):
             o_woven[k] = sbt("ob%d" % k, [P, n * PACK], BF16)
-            if k == len(PIECES) - 1:
+            if k == LAST:
                 nc.vector.tensor_copy(out=woven(o_woven[k][:]), in_=planes(o_sb[k][:]))
             else:
                 nc.scalar.copy(out=woven(o_woven[k][:]), in_=planes(o_sb[k][:]))
+        o_codes = sbt("o_codes", [P, S], I32)
+        o_scales = sbt("o_scales", [P, S], U8)
         for k, (lo, n) in enumerate(PIECES):
             tok = slice(lo, lo + n)
-            nc.vector.quantize_mx(out=oc[:, tok].bitcast(FP8X4), scales=osc[:, tok], in_=o_woven[k][:])
-        nc.sync.dma_start(out_words, oc[:])
-        for q in range(4):
-            (nc.sync if q % 2 else nc.scalar).dma_start(out_2[0, 4 * q : 4 * q + 4, :].bitcast(I32), osc[32 * q : 32 * q + 4, :].bitcast(I32))
+            nc.vector.quantize_mx(out=o_codes[:, tok].bitcast(FP8X4), scales=o_scales[:, tok], in_=o_woven[k][:])
+        nc.sync.dma_start(out_1[0].rearrange("p c r -> p (c r)").bitcast(I32), o_codes[:])
+        for q in range(QUADRANTS):
+            queue = nc.sync if q % 2 else nc.scalar
+            queue.dma_start(out_2[0, 4 * q : 4 * q + 4, :].bitcast(I32), o_scales[32 * q : 32 * q + 4, :].bitcast(I32))

from contextlib import ExitStack

import concourse.mybir as mybir

F32 = mybir.dt.float32
BF16 = mybir.dt.bfloat16
I32 = mybir.dt.int32
U32 = mybir.dt.uint32
U16 = mybir.dt.uint16
U8 = mybir.dt.uint8
FP8X4 = mybir.dt.float8_e4m3fn_x4
FP4X4 = mybir.dt.float4_e2m1fn_x4
ACT = mybir.ActivationFunctionType
ALU = mybir.AluOpType

P = 128
PACK = 4
T = 2048
S = 512
HALF = S // 2
QUARTER = S // 4
BANK = 512
QUADRANTS = 4
PIECES = ((0, HALF), (HALF, QUARTER), (HALF + QUARTER, QUARTER))
LAST = len(PIECES) - 1
VECTOR_PLANE = 0
ZEROED_BY_VECTOR = 3 * T // 4
ENGINE_COPIES = 2
FLOPS = 3 * 2 * 512 * 512 * 512


def tile_picked_logcosh2_none_po_kernel(
    tc, x_words, x_scales, w1_words, w1_scales, gn, w2_words, w2_scales, res, w3_words, w3_scales,
    offs, n1, n2, mv, out_0, out_1, out_2,
):
    nc = tc.nc
    with ExitStack() as ctx:
        sb = ctx.enter_context(tc.tile_pool(name="sb", bufs=1))
        ps = ctx.enter_context(tc.psum_pool(name="ps", bufs=1))

        def sbt(name, shape, dtype, tag=""):
            return sb.tile(shape, dtype, name=name, tag=tag, align_bytes=64)

        def bank(i, name):
            return ps.tile([P, BANK], F32, name=name, tag="bank%d" % i)

        def load_list(name, src):
            tile = sb.tile([P, S // 16], U16, name=name)
            nc.sync.dma_start(tile[:], src)
            return tile

        def load_scale_rows(tile, src):
            for q in range(QUADRANTS):
                nc.sync.dma_start(tile[32 * q : 32 * q + 4, :].bitcast(I32), src[0, 4 * q : 4 * q + 4, :].bitcast(I32))

        def load_words(name, src, tag):
            tile = sbt(name, [P, 2 * S], U8, tag)
            nc.sync.dma_start(tile[:].bitcast(I32), src[0].bitcast(I32))
            return tile

        def deal_words(name, raw, tag=""):
            words = sbt(name, [P, 2 * S], U8, tag)
            nc.vector.tensor_copy(
                out=words[:].rearrange("p (t c i b) -> p c t i b", t=PACK, i=8, b=2),
                in_=raw[:].rearrange("p (c i t b) -> p c t i b", t=PACK, i=8, b=2),
            )
            return words

        def deal_scales(name, raw, tag=""):
            scales = sbt(name, [P, S], U8, tag)
            nc.vector.tensor_copy(
                out=scales[:].rearrange("p (t m) -> p t m", t=PACK), in_=raw[:].rearrange("p (m t) -> p t m", t=PACK)
            )
            return scales

        def product(out, weight, t, codes, scales):
            words, weight_scales = weight
            nc.tensor.matmul_mx(
                out=out,
                lhsT=words[:, 2 * P * t : 2 * P * (t + 1)].bitcast(FP4X4),
                lhsT_scale=weight_scales[:, P * t : P * (t + 1)],
                rhs=codes.bitcast(FP8X4),
                rhs_scale=scales,
                start=True,
                stop=True,
            )

        def entries(lst, lo, n):
            return lst[:, lo // 16 : (lo + n) // 16]

        def plane_slots(banks, n):
            per = PACK // len(banks)
            return [banks[t // per][:, (t % per) * n : (t % per + 1) * n] for t in range(PACK)]

        def woven(ap):
            return ap.rearrange("p (c i t) -> p c t i", i=4, t=PACK)

        def planes(ap):
            return ap.rearrange("p t (c i) -> p c t i", i=4)

        xs_all = sbt("xs_all", [P, T], U8, "xs_all")
        nc.vector.memset(xs_all[:, :ZEROED_BY_VECTOR].bitcast(I32), 0)
        nc.gpsimd.memset(xs_all[:, ZEROED_BY_VECTOR:].bitcast(I32), 0)
        ws_raw = sbt("ws_raw", [P, S], U8)
        nc.gpsimd.memset(ws_raw[:].bitcast(I32), 0)
        offs_t = load_list("offs_t", offs)
        w1w_raw = load_words("w1w_raw", w1_words, "ab")
        load_scale_rows(xs_all, x_scales)
        xw_all = sbt("xw_all", [P, T], I32)
        nc.sync.dma_start(xw_all[:], x_words[0].rearrange("p c r -> p (c r)").bitcast(I32))
        load_scale_rows(ws_raw, w1_scales)
        n1_t = load_list("n1_t", n1)
        n2_t = load_list("n2_t", n2)

        y_two = [sbt("y_two%d" % t, [P, 2 * S], F32, "y_two%d" % t) for t in range(PACK)]
        y_last = sbt("y_last", [P, S], F32)
        y_own = [y_two[t + 1][:, S:] for t in range(PACK - 1)] + [y_last[:]]
        nc.vector.memset(y_two[0][:, S:], 0.0)
        w1 = (deal_words("w1w", w1w_raw), deal_scales("w1s", ws_raw))
        xs = sbt("xs", [P, S], U8)
        xw = sbt("xw", [P, S], U32)
        y_ps = {}
        for half in range(2):
            tok = slice(half * HALF, (half + 1) * HALF)
            picked = entries(offs_t, half * HALF, HALF)
            nc.vector.tensor_copy(out=xs[:, tok], in_=xs_all[:].indirect(picked))
            nc.vector.tensor_copy(out=xw[:, tok], in_=xw_all[:].bitcast(U32).indirect(picked))
            for t in range(PACK):
                y_ps[half, t] = bank(PACK * half + t, "y_ps%d_%d" % (half, t))
                product(y_ps[half, t][:, :HALF], w1, t, xw[:, tok], xs[:, tok])

        w2w = deal_words("w2w", load_words("w2w_raw", w2_words, "ab"))
        mv_t = load_list("mv_t", mv)
        load_scale_rows(ws_raw, w2_scales)
        gain = sbt("gain", [P, PACK], F32, "xs_all")
        nc.sync.dma_start(gain[:], gn.rearrange("(p t) o -> p (t o)", t=PACK))

        ab = sbt("ab", [P, PACK, 2, S], F32, "ab")
        mag = sbt("mag", [P, PACK, 2, S], F32)
        th = sbt("th", [P, PACK, 2, S], F32)
        for t in range(PACK):
            nc.scalar.copy(out=y_two[t][:, :HALF], in_=y_ps[0, t][:, :HALF])
            if t < ENGINE_COPIES:
                nc.scalar.copy(out=y_own[t][:, :HALF], in_=y_ps[0, t][:, :HALF])
            nc.scalar.copy(out=y_two[t][:, HALF:S], in_=y_ps[1, t][:, :HALF])
            if t < ENGINE_COPIES:
                nc.vector.tensor_copy(out=y_own[t][:, HALF:], in_=y_two[t][:, HALF:S])
            else:
                nc.sync.dma_start(y_own[t], y_two[t][:, :S])
        for t in range(PACK):
            parts = ((0, 0, S), (1, 0, S)) if t < PACK - 1 else ((0, 0, S), (1, 0, HALF), (1, HALF, HALF))
            for j, lo, n in parts:
                nc.vector.tensor_tensor(
                    out=ab[:, t, j, lo : lo + n],
                    in0=y_two[t][:].indirect(entries((n1_t, n2_t)[j], lo, n)),
                    in1=y_own[t][:, lo : lo + n],
                    op=ALU.subtract,
                )
            for j, lo, n in parts:
                nc.scalar.activation(out=mag[:, t, j, lo : lo + n], in_=ab[:, t, j, lo : lo + n], func=ACT.Abs)
            for j, lo, n in parts:
                nc.scalar.activation(out=th[:, t, j, lo : lo + n], in_=mag[:, t, j, lo : lo + n], func=ACT.Tanh)

        w2 = (w2w, deal_scales("w2s", ws_raw, "y_two3"))
        load_scale_rows(ws_raw, w3_scales)
        res_t = sbt("res_t", [P, PACK, S], F32, "y_two2")
        nc.sync.dma_start(res_t[:], res.rearrange("(p t) s -> p t s", t=PACK))
        w3w_raw = load_words("w3w_raw", w3_words, "y_two1")

        diff = sbt("diff", [P, PACK, S], F32)
        for lo in range(0, S, HALF):
            tok = slice(lo, lo + HALF)
            nc.vector.tensor_tensor(out=diff[:, :, tok], in0=mag[:, :, 0, tok], in1=mag[:, :, 1, tok], op=ALU.subtract)
        logs = {}

        def log_of(j, lo, n):
            logs[j, lo] = sbt("log%d_%d" % (j, lo), [P, PACK, n], F32)
            nc.scalar.activation(out=logs[j, lo][:], in_=th[:, :, j, lo : lo + n], func=ACT.Ln, bias=1.0)

        log_of(0, 0, QUARTER)
        log_of(0, QUARTER, QUARTER)
        log_of(1, *PIECES[0])
        log_of(0, HALF, HALF)
        log_of(1, *PIECES[1])
        log_of(1, *PIECES[2])
        less_a = sbt("less_a", [P, PACK, S], F32)
        h_win = [sbt("h_win%d" % t, [P, S], F32) for t in range(PACK)]
        sums, z_woven, h_ps = {}, {}, {}

        def take_log_a(lo, n):
            tok = slice(lo, lo + n)
            nc.vector.tensor_tensor(out=less_a[:, :, tok], in0=diff[:, :, tok], in1=logs[0, lo][:], op=ALU.subtract)

        def add_log_b(k):
            lo, n = PIECES[k]
            sums[k] = sbt("sum%d" % k, [P, PACK, n], F32)
            nc.vector.tensor_tensor(out=sums[k][:], in0=less_a[:, :, lo : lo + n], in1=logs[1, lo][:], op=ALU.add)

        def weave_z(k):
            lo, n = PIECES[k]
            z_woven[k] = sbt("z%d" % k, [P, n * PACK], BF16, "z%d" % k)
            gain_rows = gain[:].unsqueeze(1).unsqueeze(3).broadcast_to([P, n // 4, PACK, 4])
            nc.vector.tensor_tensor(out=woven(z_woven[k][:]), in0=planes(sums[k][:]), in1=gain_rows, op=ALU.mult)

        h_banks = ((0, 1), (2,), (3, 7))

        def second_product(k):
            lo, n = PIECES[k]
            codes = sbt("zc%d" % k, [P, n], U32)
            scales = sbt("zs%d" % k, [P, n], U8)
            nc.vector.quantize_mx(out=codes[:].bitcast(FP8X4), scales=scales[:], in_=z_woven[k][:])
            h_ps[k] = plane_slots([bank(i, "h_ps%d" % i) for i in h_banks[k]], n)
            for t in range(PACK):
                product(h_ps[k][t], w2, t, codes[:], scales[:])

        take_log_a(0, QUARTER)
        take_log_a(QUARTER, QUARTER)
        add_log_b(0)
        take_log_a(HALF, HALF)
        for k in range(len(PIECES)):
            weave_z(k)
            if k < LAST:
                add_log_b(k + 1)
            second_product(k)

        half_one = sbt("half_one", [P, 1], F32)
        nc.scalar.activation(out=half_one[:], in_=logs[1, PIECES[LAST][0]][:, 0, 0:1], func=ACT.Sigmoid, scale=0.0)

        for t in range(PACK):
            for k, (lo, n) in enumerate(PIECES):
                if t == VECTOR_PLANE:
                    nc.scalar.activation(out=h_win[t][:, lo : lo + n], in_=h_ps[k][t], func=ACT.Sigmoid, scale=2.0)
                elif k == LAST and t >= PACK // 2:
                    nc.vector.tensor_copy(out=h_win[t][:, lo : lo + n], in_=h_ps[k][t])
                else:
                    nc.scalar.copy(out=h_win[t][:, lo : lo + n], in_=h_ps[k][t])

        gain2 = sbt("gain2", [P, PACK], F32)
        nc.vector.tensor_scalar(out=gain2[:], in0=gain[:], scalar1=2.0, scalar2=None, op0=ALU.mult)
        w3 = (deal_words("w3w", w3w_raw, "z%d" % LAST), deal_scales("w3s", ws_raw))

        fetched, z2_woven, o_ps, o_sb, o_woven = {}, {}, {}, {}, {}
        for k, (lo, n) in enumerate(PIECES):
            fetched[k] = sbt("fetched%d" % k, [P, PACK, n], F32)
            for t in range(PACK):
                window = h_win[t][:].indirect(entries(mv_t, lo, n))
                if t == VECTOR_PLANE:
                    nc.vector.tensor_copy(out=fetched[k][:, t, :], in_=window)
                else:
                    nc.scalar.activation(out=fetched[k][:, t, :], in_=window, func=ACT.Sigmoid, scale=2.0)

        def weave_z2(k):
            lo, n = PIECES[k]
            z2_woven[k] = sbt("z2_%d" % k, [P, n * PACK], BF16)
            nc.vector.scalar_tensor_tensor(
                out=z2_woven[k][:].rearrange("p (s t) -> p s t", t=PACK),
                in0=fetched[k][:].rearrange("p t s -> p s t"),
                scalar=half_one[:],
                in1=gain2[:].unsqueeze(1).broadcast_to([P, n, PACK]),
                op0=ALU.subtract,
                op1=ALU.mult,
            )

        o_banks = ((4, 5), (6,), (7,))

        def third_product(k):
            lo, n = PIECES[k]
            codes = sbt("z2c%d" % k, [P, n], U32)
            scales = sbt("z2s%d" % k, [P, n], U8)
            nc.vector.quantize_mx(out=codes[:].bitcast(FP8X4), scales=scales[:], in_=z2_woven[k][:])
            o_ps[k] = [bank(i, "o_ps%d" % i) for i in o_banks[k]]
            for t, slot in enumerate(plane_slots(o_ps[k], n)):
                product(slot, w3, t, codes[:], scales[:])

        for step in range(len(PIECES) + 1):
            if step <= LAST:
                weave_z2(step)
            if step > 0:
                third_product(step - 1)

        out_rows = out_0.rearrange("(p t) s -> p t s", t=PACK)
        for k, (lo, n) in enumerate(PIECES):
            tok = slice(lo, lo + n)
            o_sb[k] = sbt("o%d" % k, [P, PACK, n], F32)
            per = BANK // n
            for i, tile in enumerate(o_ps[k]):
                rows = slice(i * per, (i + 1) * per)
                nc.vector.tensor_tensor(
                    out=o_sb[k][:, rows, :],
                    in0=tile[:].rearrange("p (t s) -> p t s", t=per),
                    in1=res_t[:, rows, tok],
                    op=ALU.add,
                )
            nc.sync.dma_start(out_rows[:, :, tok], o_sb[k][:])
        for k, (lo, n) in enumerate(PIECES):
            o_woven[k] = sbt("ob%d" % k, [P, n * PACK], BF16)
            if k == LAST:
                nc.vector.tensor_copy(out=woven(o_woven[k][:]), in_=planes(o_sb[k][:]))
            else:
                nc.scalar.copy(out=woven(o_woven[k][:]), in_=planes(o_sb[k][:]))
        o_codes = sbt("o_codes", [P, S], I32)
        o_scales = sbt("o_scales", [P, S], U8)
        for k, (lo, n) in enumerate(PIECES):
            tok = slice(lo, lo + n)
            nc.vector.quantize_mx(out=o_codes[:, tok].bitcast(FP8X4), scales=o_scales[:, tok], in_=o_woven[k][:])
        nc.sync.dma_start(out_1[0].rearrange("p c r -> p (c r)").bitcast(I32), o_codes[:])
        for q in range(QUADRANTS):
            queue = nc.sync if q % 2 else nc.scalar
            queue.dma_start(out_2[0, 4 * q : 4 * q + 4, :].bitcast(I32), o_scales[32 * q : 32 * q + 4, :].bitcast(I32))
